import numpy as np, ml_dtypes
CORES = [2,6,10,14,18,22,26,30]
N = 8
import mx_ref
BF = ml_dtypes.bfloat16
def gentries(a):
    return np.ascontiguousarray(a.reshape(8, 16, -1).transpose(0, 2, 1)).reshape(8, -1)
def gtable(e):
    e = np.asarray(e); return np.ascontiguousarray(e.reshape(8, -1, 16).transpose(0, 2, 1)).reshape(128, -1).astype(np.int32)
def gcols(t, e):
    v = np.concatenate([t.reshape(8, 16, -1, 4), np.zeros((8, 16, 1, 4), BF)], axis=2)
    return np.ascontiguousarray(np.stack([v[g][:, e[g]] for g in range(8)])).reshape(128, -1)
def gpick(z, e):
    return np.concatenate([z[16 * g:16 * g + 16][:, e[g]] for g in range(8)])
def tile(rs):
    return np.stack(rs, axis=2).reshape(128, -1).astype(BF)
def pick(q, e):
    c = np.concatenate([q[0].reshape(128, -1, 4), np.zeros((128, 1, 4), np.uint8)], axis=1); s = np.concatenate([q[1], np.ones((16, 1), np.uint8)], axis=1)
    return (np.ascontiguousarray(c[:, e].reshape(128, -1)), np.ascontiguousarray(s[:, e]))
def join(*qs):
    return (np.concatenate([q[0] for q in qs], axis=1), np.concatenate([q[1] for q in qs], axis=1))
def put(q, e, v):
    c, s = q[0].reshape(128, -1, 4).copy(), q[1].copy(); c[:, e] = v[0].reshape(128, -1, 4); s[:, e] = v[1]
    return (c.reshape(128, -1), s)
def pk(c, s):
    return (np.ascontiguousarray(c), mx_ref.live(s))
def emit(q):
    return q[0], q[1]
def packed(v, rng):
    q = [mx_ref.quantize(np.ascontiguousarray(v[r])) for r in range(N)]
    return np.stack([a for a, b in q]), np.stack([mx_ref.plane(b, rng) for a, b in q])
def values_of_codes():
    e, c = np.zeros((128, 128, 4), np.float32), np.zeros((128, 2, 4), np.uint8)
    e[np.arange(128), np.arange(128), 0] = 1
    c[:127, :, 0] = np.arange(256).reshape(2, 128).T[:127]
    return mx_ref.matmul(mx_ref.quantize(e.reshape(128, 512).astype(BF)), (c.reshape(128, 8), np.full((16, 2), 127, np.uint8))).T.reshape(-1).astype(np.float64)
CODE_VALUE, SCALE_VALUE = values_of_codes(), 2.0 ** (np.arange(256) - 127.0)
def decode(q):
    return (CODE_VALUE[q[0]].reshape(16, 8, -1, 4) * SCALE_VALUE[q[1]][:, None, :, None] + 0.0).reshape(128, -1).astype(np.float32)
def f(rng, *shape):
    return mx_ref.flush((rng.standard_normal(shape, dtype=np.float32) * np.exp2(rng.integers(-2, 3, shape[:-1] + (1,)))).astype(BF))
def wide(rng, *shape, cols=0):
    v = rng.standard_normal(shape, dtype=np.float32) * np.exp2(rng.integers(-12, 13, shape)).astype(np.float32)
    if cols: v *= np.repeat(np.exp2(rng.integers(-cols, cols + 1, shape[:-2] + (1, shape[-1] // 4))) * (rng.random(shape[:-2] + (1, shape[-1] // 4)) > 0.0625), 4, axis=-1).astype(np.float32)
    return mx_ref.flush(v.astype(BF))
C, K, A, R, SWEEPS = 320, 128, 64, 3, 4
def big(v):
    v = v.astype(np.float32)
    v[np.abs(v) < np.float32(2.0 ** -16)] = 0
    return v.astype(BF)
def numbers_of(rng):
    return {"x": big(f(rng, N, 128, 4 * C)), "u": np.array(f(rng, N, 128, 512)), "v": np.array(f(rng, N, 128, 512))}
def stored(t):
    return np.stack([gtable(np.clip(t[r], 0, C - 1)) for r in range(N)])
def received(rng):
    return stored(np.arange(C) + rng.integers(-6, 26, (N, 8, C)))
def give(rng, w):
    c, s = packed(np.ascontiguousarray(w).reshape(N, 128, 2048), rng)
    return {"wc": c, "ws": s}
def weights(rng, still=[]):
    w = np.array(mx_ref.flush((rng.standard_normal((N, 128, 2048), dtype=np.float32) * np.float32(0.25)).astype(BF))).reshape(N, 8, 16, 4, 8, 16, 4)
    for i in still:
        w[:, :, i] = 0
        w[:, :, :, :, :, i] = 0
    return give(rng, w)
def setup_inputs(rng):
    return {**numbers_of(rng), "rv": received(rng), **weights(rng)}
def setup_inputs_ties(rng):
    d = numbers_of(rng)
    x = d["x"].reshape(N, 8, 16, C, 4)
    x[:, :, 0] = 0
    x[:, :, 8] = 0
    x[:, :, 0, :, 0] = rng.integers(0, 3, (N, 8, C)).astype(np.float32).astype(BF)
    x[:, :, 8, :, 0] = rng.integers(-1, 2, (N, 8, C)).astype(np.float32).astype(BF)
    u = d["u"].reshape(N, 128, 128, 4)
    u[:, :, ::8] = 0
    o = rng.permutation(N)
    for r in range(N):
        for h in range(0, 128, 16):
            u[r, h, h, 0] = 0.0 if r == o[0] else -1.0 if r == o[1] else 1.0
            u[r, h + 8, h + 8, 0] = 1.0
    t = np.arange(C) + rng.integers(-6, 26, (N, 8, C))
    g = rng.integers(8)
    t[o[0] - 1, g - 1] = 21
    t[o[0], g, C - 1] = 1
    x[o[0], g, 8, C - 1, 0] = 1.0
    return {"x": x.reshape(N, 128, 4 * C), "u": u.reshape(N, 128, 512), "v": d["v"], "rv": stored(t), **weights(rng, [0, 8])}
def setup_inputs_near(rng):
    d = numbers_of(rng)
    x = d["x"].astype(np.float32).reshape(N, 8, 16, C, 4)
    x[:, :, 0] = 0
    x[:, :, 8:] = 0
    x[:, :, 0, :, 0] = rng.integers(0, 2, (N, 8, C)) * 2.0 - 1.0
    s = rng.integers(0, 16, (N, 8, C))
    t = rng.integers(-1, 2, (N, 8, C))
    x[:, :, 8] = ((s[:, :, :, None] >> np.arange(4)) & 1) * np.exp2(np.arange(4) - 23.0)
    x[:, :, 11, :, 0] = 2.0 ** -10
    x[:, :, 12, :, 0] = t * 2.0 ** -10
    u = d["u"].reshape(N, 128, 128, 4)
    u[:, :, ::8] = 0
    u[:, :, 8::16] = 0
    o = rng.permutation(N) % 2
    for r in range(N):
        if o[r] == 1:
            x[r, :, 8:] = 0
            x[r, :, 8, :, 0] = (s[r] - 8) * 2.0 ** -28
            x[r, :, 12, :, 0] = t[r] * 2.0 ** -28
            x[r, :, 13, :, 0] = rng.integers(0, 2, (8, C)) * 1.125 * 2.0 ** -28
            for g in rng.permutation(8)[:4]: x[r, g, 8, rng.integers(C), 0] = 2.0 ** 20 * rng.choice([-1.0, 1.0])
        for h in range(0, 128, 16):
            k = 2.0 ** -30 if o[r] == 1 else 1.0
            u[r, h + 12, h + 8, 0] = k
            if o[r] == 1:
                u[r, h + 8, h, 0] = k
                u[r, h + 13, h, 0] = k
                u[r, h + 13, h + 8, 0] = k
            else:
                u[r, h, h, 0] = k
                u[r, h + 8, h] = k
                u[r, h + 11, h, 0] = k
    return {"x": x.reshape(N, 128, 4 * C).astype(BF), "u": u.reshape(N, 128, 512), "v": d["v"], "rv": received(rng), **weights(rng, [0, 8, 9, 10, 11, 12, 13, 14, 15])}
def setup_inputs_chains(rng):
    d = numbers_of(rng)
    x = d["x"].reshape(N, 8, 16, C, 4)
    m = np.exp2(rng.integers(-12, -5, (N, 8, 8, C, 4))) * (1 + (2 * rng.integers(0, 64, (N, 8, 8, C, 4)) + 1) * 2.0 ** -7) * rng.choice([-1.0, 1.0], (N, 8, 8, C, 4))
    m[:, :, 3, :, 0] = 7.875 * rng.choice([-1.0, 1.0], (N, 8, C))
    x[:, :, :8] = m.astype(np.float32).astype(BF)
    x[:, :, 12] = 0
    x[:, :, 12, :, 0] = np.where(rng.random((N, 8, C)) < 0.0625, -1, 1).astype(np.float32).astype(BF)
    u = d["u"].reshape(N, 128, 128, 4)
    u[:, :, 8::16] = 0
    for h in range(0, 128, 16): u[:, h + 12, h + 8, 0] = 1
    t = np.arange(C) + np.zeros((N, 8, 1), np.int64)
    o = np.repeat(rng.permutation(4), 2) if N == 8 else np.concatenate([[1, 1], rng.permutation([0, 3])])
    o = np.roll(o, rng.integers(N))
    for r in range(N):
        if o[r] == 0: t[r] -= rng.integers(2, 5, (8, 1))
        elif o[r] == 1: t[r, rng.integers(8)] -= 21
        elif o[r] == 2: t[r] = C - 1
        else: t[r] += rng.integers(-30, 61, (8, C))
    return {"x": x.reshape(N, 128, 4 * C), "u": u.reshape(N, 128, 512), "v": d["v"], "rv": stored(t), **weights(rng, [12])}
def setup_inputs_ends(rng):
    d = numbers_of(rng)
    x = np.zeros((N, 8, 16, C, 4))
    u = d["u"].reshape(N, 128, 128, 4)
    w = np.full((N, 128, 2048), 0.25)
    t = np.full((N, 8, C), C - 1)
    i = np.arange(128)
    o = np.roll(np.concatenate([[3, 0], rng.permutation([1, 2])] * (N // 4)), rng.integers(N))
    for r in range(N):
        a = (0.9375 + 0.0625 * rng.integers(0, 2, (8, 16, C, 4))) * 2.0 ** 20
        c = (0.9375 + 0.0625 * rng.integers(0, 2, (128, 128, 4))) * 2.0 ** 30
        if o[r] < 2:
            x[r] = -a
            c[:, 8::16] *= 1.0 if o[r] == 0 else -1.0
            if o[r] == 1: t[r] = 0
            else:
                x[r] = -2.0 ** 20
                z = x[r].reshape(128, C, 4)
                z[:65:8] = 0
                z[:65:8, :, 0] = -((rng.permutation(C) >> np.arange(9)[:, None]) & 1) * np.exp2(11.0 + np.arange(9))[:, None]
                c[:, ::16] = 2.0 ** 30
                for g in rng.permutation(8)[:4]: c[:, 16 * g] *= -1.0
                c[:65:8, ::16, 0] = 2.0 ** 30
                w[r] = 0
                for b in range(4): w[r].reshape(128, 4, 128, 4)[i, b, i, b] = 128.0
            d["v"][r] = 2.0 ** 30
        elif o[r] == 2:
            e = np.arange(C) // 2
            x[r] = (a * rng.choice([-1.0, 1.0], (8, 1, C, 1)))[:, :, e]
            for g in range(8): c[np.arange(128) // 16 != g, 16 * g:16 * g + 16] = 0
            t[r, rng.permutation(8)[:4]] = 0
            d["v"][r] = (2.0 ** 30 * rng.choice([-1.0, 1.0], (128, 512))).astype(np.float32).astype(BF)
        else:
            x[r] = 2.0 ** -28
            c[:] = 2.0 ** -30
            w[r] = 2.0 ** -30
            d["v"][r] = 2.0 ** -30
        u[r] = c.astype(np.float32).astype(BF)
    return {"x": x.reshape(N, 128, 4 * C).astype(np.float32).astype(BF), "u": u.reshape(N, 128, 512), "v": d["v"], "rv": stored(t), **give(rng, w.astype(np.float32).astype(BF))}
def setup_inputs_spread(rng):
    d = setup_inputs(rng)
    d["x"] = big(np.clip(wide(rng, N, 128, 4 * C, cols=6).astype(np.float32), -2.0 ** 20, 2.0 ** 20))
    return d
def check_inputs(d):
    b = []
    for k, lo, hi in (("x", 2.0 ** -28, 2.0 ** 20), ("u", 2.0 ** -30, 2.0 ** 30), ("v", 2.0 ** -30, 2.0 ** 30)):
        a = np.abs(d[k].astype(np.float32))
        if not (np.isfinite(a).all() and ((a == 0) | (a >= lo) & (a <= hi)).all()): b.append("a value of " + k)
    if not ((d["rv"] >= 0) & (d["rv"] < C)).all(): b.append("an entry of rv")
    none, least, most = [emit(mx_ref.quantize(np.full((128, 16), k, np.float32).astype(BF)))[1][0, 0] for k in (0.0, 2.0 ** -30, 2.0 ** 30)]
    for r in range(N):
        if ((d["wc"][r] == 0x7F) | (d["wc"][r] == 0xFF)).any(): b.append("wc: a code that is no number")
        s = mx_ref.live(d["ws"][r])
        if ((s != none) & ((s < least) | (s > most))).any(): b.append("ws: a scale out of range")
        elif not (np.sum(np.abs(decode(pk(d["wc"][r], d["ws"][r])).astype(np.float64)).reshape(128, 512, 4), axis=(0, 2)) <= 128).all(): b.append("a column of W: its sizes")
    return b
def fall(p, b):
    for i in range(SWEEPS): p = np.minimum(p, np.roll(np.take_along_axis(b, p, axis=1), 1, axis=0))
    return p
def mean(a, b):
    return ((a.astype(np.float32) + b.astype(np.float32)) * np.float32(0.5)).astype(BF)
def reference(x, u, v, rv, wc, ws):
    qu = [mx_ref.quantize(u[r]) for r in range(N)]
    lay = [pk(wc[r], ws[r]) for r in range(N)]
    now = [x[r] for r in range(N)]
    p0 = np.zeros((8, 1), np.int64) + A + 2 * np.arange(K)
    lq = np.zeros((N, 8, K), np.float32)
    for t in range(R):
        own, order, bound, sent, line = [], [], [], [], []
        for r in range(N):
            q = mx_ref.quantize(now[r])
            own.append(decode(q).astype(BF))
            s = mx_ref.matmul(qu[r], q) + np.float32(0.0)
            o = np.argsort(-s[::16], axis=1, kind="stable")
            a = np.where(np.take_along_axis(s[8::16], o, axis=1) > 0, np.maximum(gentries(rv[r]) - 1, 0), C - 1)
            a = np.minimum.accumulate(a[:, ::-1], axis=1)[:, ::-1]
            order.append(o)
            bound.append(np.concatenate([a[:, 1:], np.full((8, 1), C - 1)], axis=1))
            line.append(fall(p0, bound[r]))
            sent.append(mx_ref.quantize(mean(gcols(own[r], np.take_along_axis(o, p0, axis=1)), gcols(own[r], np.take_along_axis(o, line[r], axis=1)))))
        for r in range(N):
            e = (r - 1) % N
            p = fall(line[e], bound[r])
            z = mx_ref.quantize(mean(decode(sent[e]), gcols(own[r], np.take_along_axis(order[r], p, axis=1))))
            hit = p[:, None, :] == np.arange(C)[:, None]
            low = np.zeros((8, C), np.int64)
            np.put_along_axis(low, order[r], np.where(hit.any(axis=2), np.argmax(hit, axis=2), K), axis=1)
            new = []
            for b in range(4):
                h = mx_ref.matmul(pick(lay[r], np.arange(128 * b, 128 * b + 128)), z) * np.float32(0.0625)
                new.append(own[r][:, b::4].astype(np.float32) + gpick(np.concatenate([h, np.zeros((128, 1), np.float32)], axis=1), low))
            now[r] = tile(new)
            lq[r] = p
    y = np.zeros((N, 128, C), np.float32)
    oc, osc = np.zeros((N, 128, 4 * C), np.uint8), np.zeros((N, 16, C), np.uint8)
    for r in range(N):
        q = mx_ref.quantize(now[r])
        y[r] = mx_ref.matmul(mx_ref.quantize(v[r]), q)
        oc[r], osc[r] = emit(q)
    return {"y": y, "lq": lq, "oc": oc, "osc": osc}

@@ -1,0 +1,408 @@
+from concourse.bass import DstId, RemoteDMATransfer, IndirectOffsetOnAxis
+from concourse.mybir import dt, AluOpType, ActivationFunctionType as AF
+
+C, K, R = 320, 128, 3
+BIG = 1e25
+M = 2048
+UNITS = [[19, 18, 17, None], [16, 15, 14, 13], [12, 11, 10, 9], [8, 7, 6, 5], [4, 3, 2, 1]]
+WIDTH = [320, 256, 192, 128, 128]
+
+F8, U8, BF, F32, I32, U16 = "float8_e4m3fn_x4", "uint8", "bfloat16", "float32", "int32", "uint16"
+SCRATCH = {}
+
+
+def _b(name, cols, dtype):
+    SCRATCH[name] = ("sbuf", [128, cols], dtype)
+
+
+def _q(name, cols):
+    _b("q" + name, cols, F8)
+    _b("s" + name, cols, U8)
+
+
+for _n, _c in (("xx", 320), ("uu", 128), ("ua", 128), ("ub", 128), ("vv", 128), ("ww", 512), ("vt", 128), ("bo", 128), ("bd", 128)):
+    _q(_n, _c)
+for _i in range(4):
+    _q("ez%d" % _i, 128)
+for _i in range(5):
+    _q("ct%d" % _i, WIDTH[_i])
+    _b("ct%d" % _i, 4 * WIDTH[_i], BF)
+for _i in range(R):
+    _q("eo%d" % _i, 128)
+    _q("ei%d" % _i, 128)
+    _b("pl%d" % _i, 8, U16)
+    SCRATCH["lp%d" % _i] = ("dram", [256, 8], U16)
+for _n, _c, _d in (
+        ("x0", 1280, BF), ("xw", 1792, BF), ("u0", 512, BF), ("v0", 512, BF),
+        ("half", 516, BF), ("zed", 516, BF), ("bot", 512, BF), ("bdt", 512, BF),
+        ("rvi", 32, I32), ("rvf", 32, F32), ("rvt", 32, F32), ("rvr", 640, F32), ("rvc", 320, BF),
+        ("mk0", 320, BF), ("mkw", 1280, BF), ("scm", 320, F32), ("scf", 320, F32), ("dsum", 320, BF), ("junk", 3072, BF),
+        ("fre", 20, F32), ("la", 20, F32), ("lb", 20, F32), ("psx", 320, F32), ("rf", 20, F32), ("rl", 20, U16),
+        ("orow", 320, F32), ("ox", 320, F32), ("ol", 80, U16), ("ar", 320, BF), ("bx", 336, BF), ("bs", 1280, BF),
+        ("fs", 1280, BF), ("fa", 512, BF), ("zr", 512, BF), ("zx", 512, F32), ("zl", 32, U16), ("et", 512, BF),
+        ("bxx", 960, F32), ("bl", 60, U16), ("tt", 960, BF), ("pls", 40, U16), ("qq", 512, BF), ("qr", 136, BF), ("qx", 128, F32), ("ql", 8, U16),
+        ("fqh", 512, F32), ("vt", 512, BF), ("fq32", 512, F32), ("e1", 128, BF), ("e2", 128, F32), ("oq", 128, F32), ("oqx", 128, F32),
+        ("xl", 32, U16), ("tb", 512, F32), ("nb", 512, BF), ("yo", 320, F32)):
+    _b(_n, _c, _d)
+ALIAS = {}
+for _buf, _d, _l in (
+        ("kf", F32, (("iprow", 320), ("eqm", 320), ("gtm", 320), ("mb", 320), ("cb", 320), ("rsm", 320), ("rst", 320), ("iota4", 320), ("grow", 512), ("dk", 128),
+                     ("c20", 20), ("cl", 20), ("n20", 20), ("n8", 8), ("na", 8), ("nb8", 8), ("icol", 4), ("gcol", 4), ("gpc", 4), ("kcol", 4))),
+        ("ki", I32, (("pidx", 4), ("pi15", 4), ("pi4", 4), ("pi5", 4), ("pi41", 4))),
+        ("kb", BF, (("idc", 320), ("drm", 320), ("p0r", 128))),
+        ("kl", U16, (("ula", 8), ("ulb", 8), ("rev8", 8), ("rev20", 20)))):
+    _o = 0
+    for _n, _c in _l:
+        ALIAS[_n] = (_buf, _o, _c)
+        _o += (_c + 15) // 16 * 16
+    _b(_buf, _o, _d)
+SCRATCH["rvd"] = ("dram", [4, 640], F32)
+for _i in range(8):
+    SCRATCH["pb%d" % _i] = ("psum", [128, 512], F32)
+
+SEMAPHORES = ["kv", "ks", "kt", "kp", "ls", "dx", "du", "dv", "dr", "dw", "drd", "dri", "dp", "db1", "db2", "db3", "db4", "dq", "do", "dy"]
+SEMAPHORES += ["ap%d" % i for i in range(R)] + ["ae%d" % i for i in range(R)]
+
+
+def rank_program(g, core, T, topo):
+    rank = T.rank_of(core)
+    if rank is None:
+        return
+    A = AluOpType
+    nxt = T.cores[(rank + 1) % len(T.cores)]
+    rid, pid, _s = topo.addr(nxt)
+    eng = topo.engines(core, nxt)[:8]
+    ne, mask = len(eng), sum(1 << e for e in eng)
+
+    queues = {"v": g.vector, "s": g.scalar, "t": g.tensor, "p": g, "y": g.sync}
+    own = {"v": "kv", "s": "ks", "t": "kt", "p": "kp"}
+    total, seen, hist = {}, {q: {} for q in queues}, {}
+
+    def wait(q, sem, val):
+        if seen[q].get(sem, 0) < val:
+            queues[q].wait_ge(T.sem[sem], val)
+            seen[q][sem] = val
+
+    def k_(name, lo=0, hi=None):
+        buf, o, n = ALIAS[name]
+        return T[buf][:, o + lo:o + (n if hi is None else hi)]
+
+    def B(name, lo=0, hi=None, ph=None):
+        if name in ALIAS:
+            buf, o, n = ALIAS[name]
+            return (buf, o + lo, o + (n if hi is None else hi), ph)
+        return (name, lo, SCRATCH[name][1][1] if hi is None else hi, ph)
+
+    def clash(a, rec):
+        return a[1] < rec[1] and rec[0] < a[2] and (a[3] is None or rec[2] is None or a[3] == rec[2])
+
+    def deps(q, rd, wr):
+        need = {}
+        for accs, w in ((rd, False), (wr, True)):
+            for a in accs:
+                bank = a[0][:2] == "pb"
+                for rec in hist.get(a[0], []):
+                    if bank and q != rec[5] or clash(a, rec) and (w or rec[3]):
+                        if q == "t" and rec[5] == "t":
+                            continue
+                        need[rec[4][0]] = max(need.get(rec[4][0], 0), rec[4][1])
+        for s in sorted(need):
+            wait(q, s, need[s])
+
+    def note(q, rd, wr, tok):
+        for a in rd:
+            hist.setdefault(a[0], []).append((a[1], a[2], a[3], False, tok, q))
+        for a in wr:
+            h = hist.setdefault(a[0], [])
+            h[:] = [x for x in h if not (a[1] <= x[0] and x[1] <= a[2] and (a[3] is None or a[3] == x[2]) and x[4] != tok)]
+            h.append((a[1], a[2], a[3], True, tok, q))
+
+    def op(q, fn, args, rd, wr, **kw):
+        deps(q, rd, wr)
+        sem = own[q]
+        fn(*args, **kw).then_inc(T.sem[sem], 1)
+        total[sem] = total.get(sem, 0) + 1
+        note(q, rd, wr, (sem, total[sem]))
+
+    def dmas(q, sem, items):
+        for o, i, rd, wr in items:
+            deps(q, rd, wr)
+            queues[q].dma_start(o, i).then_inc(T.sem[sem], 16)
+            total[sem] = total.get(sem, 0) + 16
+        for o, i, rd, wr in items:
+            note(sem, rd, wr, (sem, total[sem]))
+
+    v, s = g.vector, g.scalar
+
+    def ts(out, in0, s1, op0, wr, rd, s2=None, op1=None):
+        if op1 is None:
+            op("v", v.tensor_scalar, (out, in0, s1, None, op0), rd, wr)
+        else:
+            op("v", v.tensor_scalar, (out, in0, s1, s2, op0, op1), rd, wr)
+
+    def tt(out, a, b, o, wr, rd):
+        op("v", v.tensor_tensor, (out, a, b, o), rd, wr)
+
+    def scan(out, d0, d1, init, o0, o1, wr, rd):
+        op("v", v.tensor_tensor_scan, (out, d0, d1, init, o0, o1), rd, wr)
+
+    def cp(out, i, wr, rd):
+        op("v", v.tensor_copy, (out, i), rd, wr)
+
+    def act(out, i, func, wr, rd, **kw):
+        op("s", s.activation, (out, i, func), rd, wr, **kw)
+
+    def ms(name, lo, hi, val):
+        op("v", v.memset, (T[name][:, lo:hi], val), [], [B(name, lo, hi)])
+
+    def quant(name, tname, lo, n):
+        op("v", v.quantize_mx, (T["q" + name][:, 0:n], T["s" + name][:, 0:n], T[tname][:, lo:lo + 4 * n]),
+           [B(tname, lo, lo + 4 * n)], [B("q" + name, 0, n), B("s" + name, 0, n)])
+
+    def mm(bank, n, st, sa, mv, start=True, stop=True):
+        op("t", g.tensor.matmul_mx, (T["pb%d" % bank][:, 0:n], T["q" + st][:, sa:sa + 128], T["s" + st][:, sa:sa + 128],
+                                     T["q" + mv][:, 0:n], T["s" + mv][:, 0:n], start, stop),
+           [B("q" + st), B("s" + st), B("q" + mv), B("s" + mv)], [B("pb%d" % bank)])
+
+    def iota(name, pat, base, cm, n):
+        op("p", g.iota, (k_(name, 0, n), pat, base, cm), [], [B(name, 0, n)], allow_small_or_imprecise_dtypes=True)
+
+    def diag(out, row, n, wr, rd):
+        scan(out, k_("cb", 0, n), row, 0.0, A.add, A.max, wr, rd + [B("cb", 0, n)])
+
+    dmas("y", "dx", [(T.x0[:], T.x[:], [], [B("x0")])])
+    dmas("s", "du", [(T.u0[:], T.u[:], [], [B("u0")])])
+    dmas("y", "dr", [(T.rvi[:, 0:20], T.rv[:], [], [B("rvi", 0, 20)])])
+    dmas("y", "dw", [(T.qww[:, 0:512].bitcast(dt.uint8), T.wc[:], [], [B("qww")]), (T.sww[:, 0:512], T.ws[:], [], [B("sww")])])
+    dmas("y", "dv", [(T.v0[:], T.v[:], [], [B("v0")])])
+
+    op("p", g.iota, (k_("pidx", 0, 1), [[0, 1]], 0, 1), [], [B("pidx")])
+    iota("na", [[16, 8]], 0, 0, 8)
+    iota("nb8", [[16, 8]], 8, 0, 8)
+    iota("iprow", [[0, 20], [1, 16]], 0, 0, 320)
+    ms("half", 0, 516, 0.5)
+    op("p", g.affine_select, (T.zed[:], T.half[:], [[1, 516]], A.is_equal, 0.0, -3, -4), [B("half")], [B("zed")])
+    iota("c20", [[16, 20]], 0, 0, 20)
+    iota("grow", [[1, 8], [0, 64]], 0, 0, 512)
+    iota("iota4", [[4, 320]], 0, 0, 320)
+    iota("n20", [[-32, 20]], 623, 0, 20)
+    iota("p0r", [[2, 128]], -159, 0, 128)
+    iota("idc", [[1, 320]], -160, 0, 320)
+    iota("dk", [[4, 128]], 1280, 0, 128)
+    iota("n8", [[-16, 8]], 127, 0, 8)
+
+    def c1(name, j=0):
+        return k_(name, j, j + 1), [B(name, j, j + 1)]
+
+    def kts(o, i, s1, op0, s2=None, op1=None, extra=()):
+        ts(o[0], i[0], s1, op0, o[1], i[1] + list(extra), s2, op1)
+
+    def kw(name):
+        return k_(name), [B(name)]
+    kts(c1("pi15"), c1("pidx"), 15, A.bitwise_and)
+    kts(c1("pi5"), c1("pidx"), 5, A.arith_shift_right)
+    kts(c1("pi4"), c1("pidx"), 4, A.arith_shift_right)
+    cp(k_("ula"), k_("na"), [B("ula")], [B("na")])
+    cp(k_("ulb"), k_("nb8"), [B("ulb")], [B("nb8")])
+    cp(c1("icol")[0], c1("pi15")[0], c1("icol")[1], c1("pi15")[1])
+    cp(c1("gcol")[0], c1("pi4")[0], c1("gcol")[1], c1("pi4")[1])
+    kts(c1("pi41"), c1("pi4"), 1, A.bitwise_and)
+    cp(c1("gpc")[0], c1("pi41")[0], c1("gpc")[1], c1("pi41")[1])
+    ic, icr = c1("icol")
+    kts(c1("kcol"), c1("icol"), -float(M), A.mult, 15.0 * M, A.add)
+    kts(c1("kcol", 1), c1("icol"), -float(M), A.mult, 15.0 * M - 160.0, A.add)
+    kts(c1("kcol", 2), c1("icol"), M + 1.0, A.mult, -15.0 * M, A.add)
+    kts(c1("gpc", 1), c1("gpc"), 16.0, A.mult, ic, A.subtract, icr)
+    ko, koc = k_("kcol", 0, 1), k_("kcol", 1, 2)
+    kts(kw("eqm"), kw("iprow"), ic, A.is_equal, extra=icr)
+    kts(kw("mb"), kw("eqm"), 2 * BIG, A.mult, -BIG, A.add)
+    kts(kw("rst"), kw("iprow"), 0.0, A.is_gt, 2 * BIG, A.mult)
+    kts(kw("rsm"), kw("rst"), -BIG, A.add)
+    quant("uu", "u0", 0, 128)
+    for d, l in (("ua", "ula"), ("ub", "ulb")):
+        cp(T["q" + d][:, 0:128].bitcast(dt.uint32), T.quu[:, 0:128].bitcast(dt.uint32).indirect(k_(l)), [B("q" + d)], [B("quu"), B(l)])
+        cp(T["s" + d][:, 0:128], T.suu[:, 0:128].indirect(k_(l)), [B("s" + d)], [B("suu"), B(l)])
+
+    def late_constants():
+        for b in range(4):
+            quant("ez%d" % b, "zed", 3 - b, 128)
+        kts(kw("gtm"), kw("iprow"), ic, A.is_gt, float(M), A.mult, icr)
+        kts(kw("rst"), kw("eqm"), -1e6, A.mult)
+        tt(k_("cb"), k_("rst"), k_("gtm"), A.add, [B("cb")], [B("rst"), B("gtm")])
+        kts(kw("drm"), kw("iprow"), 0.0, A.is_gt)
+        ts(T.bot[:], k_("grow"), k_("gcol", 0, 1), A.is_equal, [B("bot")], [B("grow"), B("gcol", 0, 1)])
+        cp(T.bdt[:], T.bot[:], [B("bdt")], [B("bot")])
+        ts(T.bdt[:, 3:512:4], T.bot[:, 3:512:4], -1.0, A.mult, [B("bdt")], [B("bot")])
+        quant("bo", "bot", 0, 128)
+        quant("bd", "bdt", 0, 128)
+        kts(kw("cl"), kw("c20"), k_("kcol", 2, 3), A.add, extra=[B("kcol", 2, 3)])
+        kts(kw("rev8"), kw("n8"), ic, A.subtract, extra=icr)
+        kts(kw("rev20"), kw("n20"), k_("gpc", 1, 2), A.add, extra=[B("gpc", 1, 2)])
+
+    for i in range(5):
+        ms("ct%d" % i, 0, 4 * WIDTH[i], 0.0)
+    ms("rvi", 20, 32, 0)
+    ms("mkw", 0, 1280, 0.0)
+    ms("fre", 0, 1, 0.0)
+    ms("bx", 0, 1, -160.0)
+    ms("qr", 128, 136, 512.0)
+    ts(T.rvf[:], T.rvi[:], 1.0, A.max, [B("rvf")], [B("rvi")], -1.0, A.mult)
+    op("v", v.transpose, (T.rvt[:], T.rvf[:]), [B("rvf")], [B("rvt")])
+    dmas("y", "drd", [(T.rvd[b:b + 1, :], T.rvt[32 * b:32 * b + 20, 0:32], [B("rvt")], [("rvd", b, b + 1, None)]) for b in range(4)])
+    deps("p", [("rvd", 0, 4, None), B("pi5")], [B("rvr")])
+    g.indirect_dma_start(T.rvr[:, 0:640], None, T.rvd[:], IndirectOffsetOnAxis(ap=k_("pi5", 0, 1), axis=0), bounds_check=3, oob_is_err=True).then_inc(T.sem["dri"], 16)
+    total["dri"] = 16
+    note("dri", [("rvd", 0, 4, None), B("pi5")], [B("rvr")], ("dri", 16))
+
+    def scores():
+        mm(0, 320, "ua", 0, "xx")
+        mm(1, 320, "ub", 0, "xx")
+
+    for t in range(R):
+        quant("xx", "x0" if t == 0 else "xw", 0, 320)
+        scores()
+        for b in range(4):
+            mm(2 + b, 320, "ez%d" % b, 0, "xx") if t else None
+        tt(T.scm[:], T.pb0[:, 0:320], k_("mb"), A.min, [B("scm")], [B("pb0"), B("mb")])
+        scan(T.scf[:], k_("rsm"), T.scm[:], -BIG, A.min, A.max, [B("scf")], [B("rsm"), B("scm")])
+        if t == 0:
+            late_constants()
+            for b in range(4):
+                mm(2 + b, 320, "ez%d" % b, 0, "xx")
+        act(T.mk0[:], T.pb1[:, 0:320], AF.Sign, [B("mk0")], [B("pb1")])
+        act(T.mkw[:, 0:1280:4], T.mk0[:], AF.Copy, [B("mkw")], [B("mk0")], scale=1024.0, bias=-512.0)
+
+        def whole(b):
+            act(T.xw[:, b:1280:4], T["pb%d" % (2 + b)][:, 0:320], AF.Copy, [B("xw", 0, 1280, b)], [B("pb%d" % (2 + b))], scale=2.0)
+        whole(0)
+        off = 0
+        for i in range(5):
+            ct = "ct%d" % i
+            for k, a in enumerate(UNITS[i]):
+                if a is None:
+                    tt(T[ct][:, k:1280:4], T.scf[:], T.pb0[:, 0:320], A.is_ge, [B(ct, 0, 1280, k)], [B("scf"), B("pb0")])
+                    continue
+                n = 16 * a
+                ts(T[ct][:, k:4 * n:4], T.pb0[:, 0:n], T.scf[:, n + 15:n + 16], A.is_ge, [B(ct, 0, 4 * n, k)], [B("pb0"), B("scf")])
+                act(T.junk[:, off:off + n], T[ct][:, k:4 * n:4], AF.Copy, [B("junk", off, off + n), B("fre", a, a + 1)], [B(ct, 0, 4 * n, k)],
+                    accum_out=T.fre[:, a:a + 1])
+                off += n
+            quant(ct, ct, 0, WIDTH[i])
+            mm(6, WIDTH[i], "bd" if i == 0 else "bo", 0, ct, i == 0, i == 4)
+            if i == 0:
+                scan(T.dsum[:], k_("drm"), T.ct0[:, 3:1280:4], 0.0, A.mult, A.add, [B("dsum")], [B("drm"), B("ct0", 0, 1280, 3)])
+                tt(T.la[:], T.dsum[:, 15:320:16], k_("cl"), A.add, [B("la")], [B("dsum"), B("cl")])
+        for b in range(1, 4):
+            whole(b)
+        tt(T.lb[:], T.la[:], T.fre[:], A.subtract, [B("lb")], [B("la"), B("fre")])
+        diag(T.psx[:], T.pb6[:, 0:320], 320, [B("psx")], [B("pb6")])
+        tt(T.rf[:], T.psx[:, 15:320:16], T.lb[:], A.add, [B("rf")], [B("psx"), B("lb")])
+        cp(T.rl[:], T.rf[:], [B("rl")], [B("rf")])
+        cp(T.orow[:, 0:320].indirect(T.rl[:, 0:20]), k_("iota4"), [B("orow")], [B("iota4"), B("rl")])
+        diag(T.ox[:], T.orow[:], 320, [B("ox")], [B("orow")])
+        for b in range(4):
+            ts(T.ol[:, 20 * b:20 * b + 20], T.ox[:, 15:320:16], ko, A.subtract, [B("ol", 20 * b, 20 * b + 20)], [B("ox"), B("kcol", 0, 1)], float(b), A.add)
+        if t == 0:
+            ts(T.rvc[:], T.rvr[:, 0:640].indirect(k_("rev20")), 160.0, A.add, [B("rvc")], [B("rvr"), B("rev20")])
+        tt(T.ar[:], T.mkw[:, 0:1280].indirect(T.ol[:, 0:20]), T.rvc[:], A.min, [B("ar")], [B("mkw"), B("ol", 0, 20), B("rvc")])
+        scan(T.bx[:, 1:320], T.ar[:, 0:319], T.ar[:, 0:319], -160.0, A.max, A.max, [B("bx", 1, 320)], [B("ar")])
+        for j in (4, 3, 2, 1):
+            c = 320 * (j - 1)
+            h = 16 * j
+            dmas("y", "db%d" % j, [
+                (T.bs[h:128, c:c + 320], T.bx[0:128 - h, 0:320], [B("bx", 0, 320)], [B("bs", c, c + 320, 0)]),
+                (T.bs[0:h, c:c + 320], T.bx[128 - h:128, 0:320], [B("bx", 0, 320)], [B("bs", c, c + 320, 1)])])
+        for b in range(4):
+            w, r = [B("fs", 320 * b, 320 * b + 320)], [B("xw", 0, 1280), B("ol", 20 * b, 20 * b + 20)]
+            o, i = T.fs[:, 320 * b:320 * b + 320], T.xw[:, 0:1280].indirect(T.ol[:, 20 * b:20 * b + 20])
+            if b < 2:
+                act(o, i, AF.Copy, w, r, scale=0.5)
+            else:
+                ts(o, i, 0.5, A.mult, w, r)
+
+        for b in range(4):
+            f = 320 * b
+            act(T.fa[:, 128 * b:128 * b + 128], T.fs[:, f + 1:f + 257:2], AF.Copy, [B("fa", 128 * b, 128 * b + 128)], [B("fs", f, f + 320)])
+
+        def bs(j):
+            return T.bs[:, 320 * (j - 1):320 * j], B("bs", 320 * (j - 1), 320 * j)
+        for n, j in enumerate((4, 3, 2, 1)):
+            z = T.zr[:, 128 * n:128 * n + 128]
+            if n == 0:
+                tt(z, T.bs[:, 961:1217:2], k_("p0r"), A.max, [B("zr", 0, 128)], [bs(4)[1], B("p0r")])
+            else:
+                tt(z, bs(j)[0].indirect(T.zl[:, 8 * n - 8:8 * n]), k_("p0r"), A.max, [B("zr", 128 * n, 128 * n + 128)], [bs(j)[1], B("zl", 8 * n - 8, 8 * n), B("p0r")])
+            diag(T.zx[:, 128 * n:128 * n + 128], z, 128, [B("zx", 128 * n, 128 * n + 128)], [B("zr", 128 * n, 128 * n + 128)])
+            o, w = (T.zl[:, 8 * n:8 * n + 8], [B("zl", 8 * n, 8 * n + 8)]) if n < 3 else (T["pl%d" % t][:], [B("pl%d" % t)])
+            ts(o, T.zx[:, 128 * n + 15:128 * n + 128:16], koc, A.subtract, w, [B("zx", 128 * n, 128 * n + 128), B("kcol", 1, 2)])
+        pl = T["pl%d" % t]
+        lp = T["lp%d" % t]
+        dst = DstId(rid=rid, pnc=pid)
+        deps("p", [B("pl%d" % t)], [])
+        g.remote_dma_fused([RemoteDMATransfer(dst_ids=[dst, dst], dma_engine_mask=mask, remote_sem=T.sem["ap%d" % t], srcs=[pl[:]], dsts=[lp[0:128, :], lp[128:256, :]])],
+                           local_sem=T.sem.ls)
+        note("ap%d" % t, [], [B("lp%d" % t, 0, 8)], ("ap%d" % t, 2 * ne))
+        total["ap%d" % t] = 2 * ne
+        for b in range(4):
+            f = 320 * b
+            tt(T.et[:, b:512:4], T.fs[:, f:f + 320].indirect(pl[:, 0:8]), T.fa[:, 128 * b:128 * b + 128], A.add, [B("et", 0, 512, b)], [B("fs", f, f + 320), B("fa", 128 * b, 128 * b + 128), B("pl%d" % t)])
+        quant("eo%d" % t, "et", 0, 128)
+        qo, so = "qeo%d" % t, "seo%d" % t
+        deps("p", [B(qo), B(so)], [])
+        g.remote_dma(T["qei%d" % t][:, 0:128].bitcast(dt.uint8), T[qo][:, 0:128].bitcast(dt.uint8), T.sem["ae%d" % t], T.sem.ls, pid, rid, mask)
+        g.remote_dma(T["sei%d" % t][:, 0:128], T[so][:, 0:128], T.sem["ae%d" % t], T.sem.ls, pid, rid, mask)
+        note("ae%d" % t, [], [B("qei%d" % t), B("sei%d" % t)], ("ae%d" % t, 2 * ne))
+        total["ae%d" % t] = 2 * ne
+        total["ls"] = total.get("ls", 0) + 3 * ne
+        for n, j in enumerate((2, 3, 4)):
+            diag(T.bxx[:, 320 * n:320 * n + 320], bs(j)[0], 320, [B("bxx", 320 * n, 320 * n + 320)], [bs(j)[1]])
+            ts(T.bl[:, 20 * n:20 * n + 20], T.bxx[:, 320 * n + 15:320 * n + 320:16], koc, A.subtract, [B("bl", 20 * n, 20 * n + 20)], [B("bxx", 320 * n, 320 * n + 320), B("kcol", 1, 2)])
+            src, sr = bs(1) if n == 0 else (T.tt[:, 320 * n - 320:320 * n], B("tt", 320 * n - 320, 320 * n))
+            act(T.tt[:, 320 * n:320 * n + 320], src.indirect(T.bl[:, 20 * n:20 * n + 20]), AF.Copy, [B("tt", 320 * n, 320 * n + 320)], [sr, B("bl", 20 * n, 20 * n + 20)])
+        dmas("y", "dp", [(T.pls[:, 8 * j:8 * j + 8], lp[128 - 16 * j:256 - 16 * j, :], [B("lp%d" % t)], [B("pls", 8 * j, 8 * j + 8)]) for j in range(5)])
+        for b in range(4):
+            mm(2 + b, 128, "ez%d" % b, 0, "ei%d" % t)
+        prev = None
+        for n, (src, sr) in enumerate(((T.tt[:, 640:960], B("tt", 640, 960)), (T.tt[:, 320:640], B("tt", 320, 640)), (T.tt[:, 0:320], B("tt", 0, 320)), bs(1), (k_("idc"), B("idc")))):
+            l = 8 * (4 - n)
+            o, w = (T.qq[:, 128 * n:128 * n + 128], B("qq", 128 * n, 128 * n + 128)) if n < 4 else (T.qr[:, 0:128], B("qr", 0, 128))
+            i = src.indirect(T.pls[:, l:l + 8])
+            if prev is None:
+                cp(o, i, [w], [sr, B("pls", l, l + 8)])
+            else:
+                tt(o, i, prev[0], A.max, [w], [sr, B("pls", l, l + 8), prev[1]])
+            prev = (o, w)
+        diag(T.qx[:], T.qr[:, 0:128], 128, [B("qx")], [B("qr", 0, 128)])
+        ts(T.ql[:], T.qx[:, 15:128:16], koc, A.subtract, [B("ql")], [B("qx"), B("kcol", 1, 2)])
+        for b in range(4):
+            act(T.fqh[:, 128 * b:128 * b + 128], T.fs[:, 320 * b:320 * b + 320].indirect(T.ql[:, 0:8]), AF.Copy, [B("fqh", 128 * b, 128 * b + 128)], [B("fs", 320 * b, 320 * b + 320), B("ql")])
+        tt(T.e1[:], T.qr[:, 0:128], T.qr[:, 1:129], A.is_equal, [B("e1")], [B("qr", 0, 129)])
+        tt(T.e2[:], T.e1[:], k_("dk"), A.mult, [B("e2")], [B("e1"), B("dk")])
+        for b in range(4):
+            tt(T.vt[:, b:512:4], T["pb%d" % (2 + b)][:, 0:128], T.fqh[:, 128 * b:128 * b + 128], A.add, [B("vt", 0, 512, b)], [B("pb%d" % (2 + b)), B("fqh", 128 * b, 128 * b + 128)])
+        quant("vt", "vt", 0, 128)
+        for b in range(4):
+            mm(2 + b, 128, "ww", 128 * b, "vt")
+        act(T.fq32[:], T.fqh[:], AF.Copy, [B("fq32")], [B("fqh")], scale=32.0)
+        tt(T.oq[:], T.orow[:, 0:320].indirect(T.ql[:, 0:8]), T.e2[:], A.max, [B("oq")], [B("orow"), B("ql"), B("e2")])
+        diag(T.oqx[:], T.oq[:], 128, [B("oqx")], [B("oq")])
+        for b in range(4):
+            ts(T.xl[:, 8 * b:8 * b + 8], T.oqx[:, 15:128:16], ko, A.subtract, [B("xl", 8 * b, 8 * b + 8)], [B("oqx"), B("kcol", 0, 1)], float(b), A.add)
+        for b in range(4):
+            d = slice(128 * b, 128 * b + 128)
+            tt(T.tb[:, d], T["pb%d" % (2 + b)][:, 0:128], T.fq32[:, d], A.add, [B("tb", d.start, d.stop)], [B("pb%d" % (2 + b)), B("fq32")])
+            act(T.nb[:, d], T.tb[:, d], AF.Copy, [B("nb", d.start, d.stop)], [B("tb", d.start, d.stop)], scale=0.0625)
+        cp(T.xw[:, 0:1792].indirect(T.xl[:, 0:32]), T.nb[:], [B("xw")], [B("nb"), B("xl")])
+        if t == 0:
+            quant("vv", "v0", 0, 128)
+
+    quant("xx", "xw", 0, 320)
+    mm(0, 320, "vv", 0, "xx")
+    ts(T.tb[:, 0:128], T.qr[:, 0:128].indirect(k_("rev8")), -1.0, A.mult, [B("tb", 0, 128)], [B("qr", 0, 128), B("rev8")], 159.0, A.add)
+    dmas("y", "do", [(T.oc[:], T.qxx[:, 0:320].bitcast(dt.uint8), [B("qxx")], [])]
+         + [(T.osc[4 * k:4 * k + 4, :], T.sxx[32 * k:32 * k + 4, 0:320], [B("sxx")], []) for k in range(4)]
+         + [(T.lq[:], T.tb[0:128:16, 0:128], [B("tb", 0, 128)], [])])
+    act(T.yo[:], T.pb0[:, 0:320], AF.Copy, [B("yo")], [B("pb0")])
+    dmas("s", "dy", [(T.y[:], T.yo[:], [B("yo")], [])])
+    for sem in sorted(total):
+        wait("p", sem, total[sem])

@@ -36,10 +36,10 @@ for _n, _c, _d in (
         ("x0", 1280, BF), ("xw", 1792, BF), ("u0", 512, BF), ("v0", 512, BF),
         ("half", 516, BF), ("zed", 516, BF), ("bot", 512, BF), ("bdt", 512, BF),
         ("rvi", 32, I32), ("rvf", 32, F32), ("rvt", 32, F32), ("rvr", 640, F32), ("rvc", 320, BF),
-        ("mk0", 320, BF), ("mkw", 1280, BF), ("scm", 320, F32), ("scf", 320, F32), ("dsum", 320, BF), ("junk", 3072, BF),
-        ("fre", 20, F32), ("la", 20, F32), ("lb", 20, F32), ("psx", 320, F32), ("rf", 20, F32), ("rl", 20, U16),
-        ("orow", 320, F32), ("ox", 320, F32), ("ol", 80, U16), ("ar", 320, BF), ("bx", 336, BF), ("bs", 1280, BF),
-        ("fs", 1280, BF), ("fa", 512, BF), ("zr", 512, BF), ("zx", 512, F32), ("zl", 32, U16), ("et", 512, BF),
+        ("mk0", 320, BF), ("mk1", 320, BF), ("scm", 320, F32), ("scf", 320, F32), ("dsum", 320, BF), ("junk", 3072, BF),
+        ("fre", 20, F32), ("li", 192, F32), ("dg", 960, F32), ("rl", 64, U16),
+        ("orow", 320, F32), ("ol", 80, U16), ("ar", 640, BF), ("bx", 336, BF), ("bs", 1280, BF),
+        ("fs", 1280, BF), ("fa", 512, BF), ("zr", 640, BF), ("zx", 512, F32), ("zl", 32, U16), ("et", 512, BF),
         ("bxx", 960, F32), ("bl", 60, U16), ("tt", 960, BF), ("pls", 40, U16), ("qq", 512, BF), ("qr", 136, BF), ("qx", 128, F32), ("ql", 8, U16),
         ("fqh", 512, F32), ("vt", 512, BF), ("fq32", 512, F32), ("e1", 128, BF), ("e2", 128, F32), ("oq", 128, F32), ("oqx", 128, F32),
         ("xl", 32, U16), ("tb", 512, F32), ("nb", 512, BF), ("yo", 320, F32)):
@@ -49,7 +49,7 @@ for _buf, _d, _l in (
         ("kf", F32, (("iprow", 320), ("eqm", 320), ("gtm", 320), ("mb", 320), ("cb", 320), ("rsm", 320), ("rst", 320), ("iota4", 320), ("grow", 512), ("dk", 128),
                      ("c20", 20), ("cl", 20), ("n20", 20), ("n8", 8), ("na", 8), ("nb8", 8), ("icol", 4), ("gcol", 4), ("gpc", 4), ("kcol", 4))),
         ("ki", I32, (("pidx", 4), ("pi15", 4), ("pi4", 4), ("pi5", 4), ("pi41", 4))),
-        ("kb", BF, (("idc", 320), ("drm", 320), ("p0r", 128))),
+        ("kb", BF, (("idc", 320), ("drm", 320), ("p0r", 128), ("neg", 320))),
         ("kl", U16, (("ula", 8), ("ulb", 8), ("rev8", 8), ("rev20", 20)))):
     _o = 0
     for _n, _c in _l:
@@ -181,15 +181,15 @@ def rank_program(g, core, T, topo):
     iota("nb8", [[16, 8]], 8, 0, 8)
     iota("iprow", [[0, 20], [1, 16]], 0, 0, 320)
     ms("half", 0, 516, 0.5)
+    iota("grow", [[1, 8], [0, 64]], 0, 0, 512)
     op("p", g.affine_select, (T.zed[:], T.half[:], [[1, 516]], A.is_equal, 0.0, -3, -4), [B("half")], [B("zed")])
     iota("c20", [[16, 20]], 0, 0, 20)
-    iota("grow", [[1, 8], [0, 64]], 0, 0, 512)
-    iota("iota4", [[4, 320]], 0, 0, 320)
     iota("n20", [[-32, 20]], 623, 0, 20)
+    iota("n8", [[-16, 8]], 127, 0, 8)
+    iota("iota4", [[4, 320]], 0, 0, 320)
     iota("p0r", [[2, 128]], -159, 0, 128)
     iota("idc", [[1, 320]], -160, 0, 320)
     iota("dk", [[4, 128]], 1280, 0, 128)
-    iota("n8", [[-16, 8]], 127, 0, 8)
 
     def c1(name, j=0):
         return k_(name, j, j + 1), [B(name, j, j + 1)]
@@ -215,37 +215,34 @@ def rank_program(g, core, T, topo):
     kts(c1("gpc", 1), c1("gpc"), 16.0, A.mult, ic, A.subtract, icr)
     ko, koc = k_("kcol", 0, 1), k_("kcol", 1, 2)
     kts(kw("eqm"), kw("iprow"), ic, A.is_equal, extra=icr)
-    kts(kw("mb"), kw("eqm"), 2 * BIG, A.mult, -BIG, A.add)
-    kts(kw("rst"), kw("iprow"), 0.0, A.is_gt, 2 * BIG, A.mult)
-    kts(kw("rsm"), kw("rst"), -BIG, A.add)
+    kts(kw("drm"), kw("iprow"), 0.0, A.is_gt)
+    kts(kw("gtm"), kw("iprow"), ic, A.is_gt, float(M), A.mult, icr)
+    act(k_("rst"), k_("eqm"), AF.Copy, [B("rst")], [B("eqm")], scale=-1e6)
+    act(k_("mb"), k_("eqm"), AF.Copy, [B("mb")], [B("eqm")], scale=2 * BIG, bias=-BIG)
+    act(k_("rsm"), k_("drm"), AF.Copy, [B("rsm")], [B("drm")], scale=2 * BIG, bias=-BIG)
+    for i in range(5):
+        ms("ct%d" % i, 64 * min(a for a in UNITS[i] if a), 4 * WIDTH[i], 0.0)
+    ts(T.bot[:], k_("grow"), k_("gcol", 0, 1), A.is_equal, [B("bot")], [B("grow"), B("gcol", 0, 1)])
+    act(T.bdt[:], T.bot[:], AF.Copy, [B("bdt")], [B("bot")])
+    act(T.bdt[:, 3:512:4], T.bot[:, 3:512:4], AF.Copy, [B("bdt")], [B("bot")], scale=-1.0)
     quant("uu", "u0", 0, 128)
     for d, l in (("ua", "ula"), ("ub", "ulb")):
         cp(T["q" + d][:, 0:128].bitcast(dt.uint32), T.quu[:, 0:128].bitcast(dt.uint32).indirect(k_(l)), [B("q" + d)], [B("quu"), B(l)])
-        cp(T["s" + d][:, 0:128], T.suu[:, 0:128].indirect(k_(l)), [B("s" + d)], [B("suu"), B(l)])
+        act(T["s" + d][:, 0:128], T.suu[:, 0:128].indirect(k_(l)), AF.Copy, [B("s" + d)], [B("suu"), B(l)])
 
     def late_constants():
-        for b in range(4):
-            quant("ez%d" % b, "zed", 3 - b, 128)
-        kts(kw("gtm"), kw("iprow"), ic, A.is_gt, float(M), A.mult, icr)
-        kts(kw("rst"), kw("eqm"), -1e6, A.mult)
         tt(k_("cb"), k_("rst"), k_("gtm"), A.add, [B("cb")], [B("rst"), B("gtm")])
-        kts(kw("drm"), kw("iprow"), 0.0, A.is_gt)
-        ts(T.bot[:], k_("grow"), k_("gcol", 0, 1), A.is_equal, [B("bot")], [B("grow"), B("gcol", 0, 1)])
-        cp(T.bdt[:], T.bot[:], [B("bdt")], [B("bot")])
-        ts(T.bdt[:, 3:512:4], T.bot[:, 3:512:4], -1.0, A.mult, [B("bdt")], [B("bot")])
         quant("bo", "bot", 0, 128)
         quant("bd", "bdt", 0, 128)
         kts(kw("cl"), kw("c20"), k_("kcol", 2, 3), A.add, extra=[B("kcol", 2, 3)])
         kts(kw("rev8"), kw("n8"), ic, A.subtract, extra=icr)
         kts(kw("rev20"), kw("n20"), k_("gpc", 1, 2), A.add, extra=[B("gpc", 1, 2)])
+        ms("fre", 0, 1, 0.0)
+        ms("bx", 0, 1, -160.0)
+        ms("qr", 128, 136, 512.0)
+        op("v", v.memset, (k_("neg"), -512.0), [], [B("neg")])
 
-    for i in range(5):
-        ms("ct%d" % i, 0, 4 * WIDTH[i], 0.0)
     ms("rvi", 20, 32, 0)
-    ms("mkw", 0, 1280, 0.0)
-    ms("fre", 0, 1, 0.0)
-    ms("bx", 0, 1, -160.0)
-    ms("qr", 128, 136, 512.0)
     ts(T.rvf[:], T.rvi[:], 1.0, A.max, [B("rvf")], [B("rvi")], -1.0, A.mult)
     op("v", v.transpose, (T.rvt[:], T.rvf[:]), [B("rvf")], [B("rvt")])
     dmas("y", "drd", [(T.rvd[b:b + 1, :], T.rvt[32 * b:32 * b + 20, 0:32], [B("rvt")], [("rvd", b, b + 1, None)]) for b in range(4)])
@@ -261,24 +258,37 @@ def rank_program(g, core, T, topo):
     for t in range(R):
         quant("xx", "x0" if t == 0 else "xw", 0, 320)
         scores()
-        for b in range(4):
-            mm(2 + b, 320, "ez%d" % b, 0, "xx") if t else None
-        tt(T.scm[:], T.pb0[:, 0:320], k_("mb"), A.min, [B("scm")], [B("pb0"), B("mb")])
-        scan(T.scf[:], k_("rsm"), T.scm[:], -BIG, A.min, A.max, [B("scf")], [B("rsm"), B("scm")])
         if t == 0:
             late_constants()
-            for b in range(4):
-                mm(2 + b, 320, "ez%d" % b, 0, "xx")
+        tt(T.scm[:], T.pb0[:, 0:320], k_("mb"), A.min, [B("scm")], [B("pb0"), B("mb")])
+        if t == 0:
+            for b in range(2):
+                quant("ez%d" % b, "zed", 3 - b, 128)
+        scan(T.scf[:], k_("rsm"), T.scm[:], -BIG, A.min, A.max, [B("scf")], [B("rsm"), B("scm")])
+        if t == 0:
+            for b in range(2, 4):
+                quant("ez%d" % b, "zed", 3 - b, 128)
+        for b in range(4):
+            mm(2 + b, 320, "ez%d" % b, 0, "xx")
         act(T.mk0[:], T.pb1[:, 0:320], AF.Sign, [B("mk0")], [B("pb1")])
-        act(T.mkw[:, 0:1280:4], T.mk0[:], AF.Copy, [B("mkw")], [B("mk0")], scale=1024.0, bias=-512.0)
+        act(T.mk1[:], T.mk0[:], AF.Relu, [B("mk1")], [B("mk0")])
 
         def whole(b):
             act(T.xw[:, b:1280:4], T["pb%d" % (2 + b)][:, 0:320], AF.Copy, [B("xw", 0, 1280, b)], [B("pb%d" % (2 + b))], scale=2.0)
         whole(0)
         off = 0
+
+        def li(j):
+            return T.li[:, 32 * j:32 * j + 20], B("li", 32 * j, 32 * j + 20)
+
+        def count(i):
+            quant("ct%d" % i, "ct%d" % i, 0, WIDTH[i])
+            mm(6, WIDTH[i], "bd" if i == 0 else "bo", 0, "ct%d" % i, i == 0, i == 4)
         for i in range(5):
             ct = "ct%d" % i
             for k, a in enumerate(UNITS[i]):
+                if i and k == 1:
+                    count(i - 1)
                 if a is None:
                     tt(T[ct][:, k:1280:4], T.scf[:], T.pb0[:, 0:320], A.is_ge, [B(ct, 0, 1280, k)], [B("scf"), B("pb0")])
                     continue
@@ -287,54 +297,82 @@ def rank_program(g, core, T, topo):
                 act(T.junk[:, off:off + n], T[ct][:, k:4 * n:4], AF.Copy, [B("junk", off, off + n), B("fre", a, a + 1)], [B(ct, 0, 4 * n, k)],
                     accum_out=T.fre[:, a:a + 1])
                 off += n
-            quant(ct, ct, 0, WIDTH[i])
-            mm(6, WIDTH[i], "bd" if i == 0 else "bo", 0, ct, i == 0, i == 4)
-            if i == 0:
+            if i == 1:
                 scan(T.dsum[:], k_("drm"), T.ct0[:, 3:1280:4], 0.0, A.mult, A.add, [B("dsum")], [B("drm"), B("ct0", 0, 1280, 3)])
-                tt(T.la[:], T.dsum[:, 15:320:16], k_("cl"), A.add, [B("la")], [B("dsum"), B("cl")])
-        for b in range(1, 4):
-            whole(b)
-        tt(T.lb[:], T.la[:], T.fre[:], A.subtract, [B("lb")], [B("la"), B("fre")])
-        diag(T.psx[:], T.pb6[:, 0:320], 320, [B("psx")], [B("pb6")])
-        tt(T.rf[:], T.psx[:, 15:320:16], T.lb[:], A.add, [B("rf")], [B("psx"), B("lb")])
-        cp(T.rl[:], T.rf[:], [B("rl")], [B("rf")])
-        cp(T.orow[:, 0:320].indirect(T.rl[:, 0:20]), k_("iota4"), [B("orow")], [B("iota4"), B("rl")])
-        diag(T.ox[:], T.orow[:], 320, [B("ox")], [B("orow")])
-        for b in range(4):
-            ts(T.ol[:, 20 * b:20 * b + 20], T.ox[:, 15:320:16], ko, A.subtract, [B("ol", 20 * b, 20 * b + 20)], [B("ox"), B("kcol", 0, 1)], float(b), A.add)
+            if i == 2:
+                tt(li(0)[0], T.dsum[:, 15:320:16], k_("cl"), A.add, [li(0)[1]], [B("dsum"), B("cl")])
+        diag(T.dg[:, 320:640], T.mk1[:], 320, [B("dg", 320, 640)], [B("mk1")])
+        count(4)
         if t == 0:
             ts(T.rvc[:], T.rvr[:, 0:640].indirect(k_("rev20")), 160.0, A.add, [B("rvc")], [B("rvr"), B("rev20")])
-        tt(T.ar[:], T.mkw[:, 0:1280].indirect(T.ol[:, 0:20]), T.rvc[:], A.min, [B("ar")], [B("mkw"), B("ol", 0, 20), B("rvc")])
-        scan(T.bx[:, 1:320], T.ar[:, 0:319], T.ar[:, 0:319], -160.0, A.max, A.max, [B("bx", 1, 320)], [B("ar")])
+        act(T.ar[:, 0:320], T.rvc[:], AF.Copy, [B("ar", 0, 320)], [B("rvc")])
+        for b in range(1, 4):
+            whole(b)
+        ts(li(3)[0], T.dg[:, 335:640:16], ko, A.subtract, [li(3)[1]], [B("dg", 320, 640), B("kcol", 0, 1)], 320.0, A.mult)
+        tt(li(1)[0], li(0)[0], T.fre[:], A.subtract, [li(1)[1]], [li(0)[1], B("fre")])
+        tt(li(2)[0], li(1)[0], li(3)[0], A.add, [li(2)[1]], [li(1)[1], li(3)[1]])
+        diag(T.dg[:, 0:320], T.pb6[:, 0:320], 320, [B("dg", 0, 320)], [B("pb6")])
+        tt(li(4)[0], T.dg[:, 15:320:16], li(2)[0], A.add, [li(4)[1]], [B("dg", 0, 320), li(2)[1]])
+        tt(li(5)[0], T.dg[:, 15:320:16], li(1)[0], A.add, [li(5)[1]], [B("dg", 0, 320), li(1)[1]])
+        cp(T.rl[:, 32:52], li(4)[0], [B("rl", 32, 52)], [li(4)[1]])
+        cp(T.rl[:, 0:20], li(5)[0], [B("rl", 0, 20)], [li(5)[1]])
+        cp(T.ar[:, 0:640].indirect(T.rl[:, 32:52]), k_("neg"), [B("ar")], [B("neg"), B("rl", 32, 52)])
+        scan(T.bx[:, 1:320], T.ar[:, 0:319], T.ar[:, 0:319], -160.0, A.max, A.max, [B("bx", 1, 320)], [B("ar", 0, 320)])
         for j in (4, 3, 2, 1):
             c = 320 * (j - 1)
             h = 16 * j
             dmas("y", "db%d" % j, [
                 (T.bs[h:128, c:c + 320], T.bx[0:128 - h, 0:320], [B("bx", 0, 320)], [B("bs", c, c + 320, 0)]),
                 (T.bs[0:h, c:c + 320], T.bx[128 - h:128, 0:320], [B("bx", 0, 320)], [B("bs", c, c + 320, 1)])])
+        cp(T.orow[:, 0:320].indirect(T.rl[:, 0:20]), k_("iota4"), [B("orow")], [B("iota4"), B("rl", 0, 20)])
+        diag(T.dg[:, 640:960], T.orow[:], 320, [B("dg", 640, 960)], [B("orow")])
         for b in range(4):
-            w, r = [B("fs", 320 * b, 320 * b + 320)], [B("xw", 0, 1280), B("ol", 20 * b, 20 * b + 20)]
-            o, i = T.fs[:, 320 * b:320 * b + 320], T.xw[:, 0:1280].indirect(T.ol[:, 20 * b:20 * b + 20])
-            if b < 2:
-                act(o, i, AF.Copy, w, r, scale=0.5)
-            else:
-                ts(o, i, 0.5, A.mult, w, r)
+            ts(T.ol[:, 20 * b:20 * b + 20], T.dg[:, 655:960:16], ko, A.subtract, [B("ol", 20 * b, 20 * b + 20)], [B("dg", 640, 960), B("kcol", 0, 1)], float(b), A.add)
 
-        for b in range(4):
+        def ordered(b):
             f = 320 * b
+            act(T.fs[:, f:f + 320], T.xw[:, 0:1280].indirect(T.ol[:, 20 * b:20 * b + 20]), AF.Copy, [B("fs", f, f + 320)], [B("xw", 0, 1280), B("ol", 20 * b, 20 * b + 20)], scale=0.5)
             act(T.fa[:, 128 * b:128 * b + 128], T.fs[:, f + 1:f + 257:2], AF.Copy, [B("fa", 128 * b, 128 * b + 128)], [B("fs", f, f + 320)])
 
         def bs(j):
             return T.bs[:, 320 * (j - 1):320 * j], B("bs", 320 * (j - 1), 320 * j)
-        for n, j in enumerate((4, 3, 2, 1)):
-            z = T.zr[:, 128 * n:128 * n + 128]
-            if n == 0:
-                tt(z, T.bs[:, 961:1217:2], k_("p0r"), A.max, [B("zr", 0, 128)], [bs(4)[1], B("p0r")])
-            else:
-                tt(z, bs(j)[0].indirect(T.zl[:, 8 * n - 8:8 * n]), k_("p0r"), A.max, [B("zr", 128 * n, 128 * n + 128)], [bs(j)[1], B("zl", 8 * n - 8, 8 * n), B("p0r")])
-            diag(T.zx[:, 128 * n:128 * n + 128], z, 128, [B("zx", 128 * n, 128 * n + 128)], [B("zr", 128 * n, 128 * n + 128)])
-            o, w = (T.zl[:, 8 * n:8 * n + 8], [B("zl", 8 * n, 8 * n + 8)]) if n < 3 else (T["pl%d" % t][:], [B("pl%d" % t)])
+        def table_row(n, j):
+            diag(T.bxx[:, 320 * n:320 * n + 320], bs(j)[0], 320, [B("bxx", 320 * n, 320 * n + 320)], [bs(j)[1]])
+
+        def table_list(n):
+            ts(T.bl[:, 20 * n:20 * n + 20], T.bxx[:, 320 * n + 15:320 * n + 320:16], koc, A.subtract, [B("bl", 20 * n, 20 * n + 20)], [B("bxx", 320 * n, 320 * n + 320), B("kcol", 1, 2)])
+
+        def compose(n):
+            src, sr = bs(1) if n == 0 else (T.tt[:, 320 * n - 320:320 * n], B("tt", 320 * n - 320, 320 * n))
+            act(T.tt[:, 320 * n:320 * n + 320], src.indirect(T.bl[:, 20 * n:20 * n + 20]), AF.Copy, [B("tt", 320 * n, 320 * n + 320)], [sr, B("bl", 20 * n, 20 * n + 20)])
+
+        def zrow(n):
+            return T.zr[:, 128 * n:128 * n + 128], B("zr", 128 * n, 128 * n + 128)
+
+        def zdiag(n):
+            diag(T.zx[:, 128 * n:128 * n + 128], zrow(n)[0], 128, [B("zx", 128 * n, 128 * n + 128)], [zrow(n)[1]])
+
+        def zlist(n):
+            o, w = (T.zl[:, 8 * n:8 * n + 8], [B("zl", 8 * n, 8 * n + 8)]) if n < 2 else (T["pl%d" % t][:], [B("pl%d" % t)])
             ts(o, T.zx[:, 128 * n + 15:128 * n + 128:16], koc, A.subtract, w, [B("zx", 128 * n, 128 * n + 128), B("kcol", 1, 2)])
+        p0 = (k_("p0r"), B("p0r"))
+        ordered(0)
+        ordered(1)
+        tt(zrow(0)[0], T.bs[:, 961:1217:2], p0[0], A.max, [zrow(0)[1]], [bs(4)[1], p0[1]])
+        table_row(0, 2)
+        zdiag(0)
+        table_list(0)
+        compose(0)
+        ordered(2)
+        ordered(3)
+        zlist(0)
+        tt(zrow(3)[0], T.bs[:, 1:257:2], p0[0], A.max, [zrow(3)[1]], [bs(1)[1], p0[1]])
+        tt(zrow(1)[0], bs(3)[0].indirect(T.zl[:, 0:8]), p0[0], A.max, [zrow(1)[1]], [bs(3)[1], B("zl", 0, 8), p0[1]])
+        zdiag(1)
+        zlist(1)
+        tt(zrow(2)[0], T.tt[:, 0:320].indirect(T.zl[:, 8:16]), zrow(3)[0], A.max, [zrow(2)[1]], [B("tt", 0, 320), B("zl", 8, 16), zrow(3)[1]])
+        zdiag(2)
+        zlist(2)
         pl = T["pl%d" % t]
         lp = T["lp%d" % t]
         dst = DstId(rid=rid, pnc=pid)
@@ -354,11 +392,13 @@ def rank_program(g, core, T, topo):
         note("ae%d" % t, [], [B("qei%d" % t), B("sei%d" % t)], ("ae%d" % t, 2 * ne))
         total["ae%d" % t] = 2 * ne
         total["ls"] = total.get("ls", 0) + 3 * ne
-        for n, j in enumerate((2, 3, 4)):
-            diag(T.bxx[:, 320 * n:320 * n + 320], bs(j)[0], 320, [B("bxx", 320 * n, 320 * n + 320)], [bs(j)[1]])
-            ts(T.bl[:, 20 * n:20 * n + 20], T.bxx[:, 320 * n + 15:320 * n + 320:16], koc, A.subtract, [B("bl", 20 * n, 20 * n + 20)], [B("bxx", 320 * n, 320 * n + 320), B("kcol", 1, 2)])
-            src, sr = bs(1) if n == 0 else (T.tt[:, 320 * n - 320:320 * n], B("tt", 320 * n - 320, 320 * n))
-            act(T.tt[:, 320 * n:320 * n + 320], src.indirect(T.bl[:, 20 * n:20 * n + 20]), AF.Copy, [B("tt", 320 * n, 320 * n + 320)], [sr, B("bl", 20 * n, 20 * n + 20)])
+        table_row(1, 3)
+        table_row(2, 4)
+        for n in (1, 2):
+            table_list(n)
+            compose(n)
+        if t == 0:
+            quant("vv", "v0", 0, 128)
         dmas("y", "dp", [(T.pls[:, 8 * j:8 * j + 8], lp[128 - 16 * j:256 - 16 * j, :], [B("lp%d" % t)], [B("pls", 8 * j, 8 * j + 8)]) for j in range(5)])
         for b in range(4):
             mm(2 + b, 128, "ez%d" % b, 0, "ei%d" % t)
@@ -373,10 +413,15 @@ def rank_program(g, core, T, topo):
                 tt(o, i, prev[0], A.max, [w], [sr, B("pls", l, l + 8), prev[1]])
             prev = (o, w)
         diag(T.qx[:], T.qr[:, 0:128], 128, [B("qx")], [B("qr", 0, 128)])
+        tt(T.e1[:], T.qr[:, 0:128], T.qr[:, 1:129], A.is_equal, [B("e1")], [B("qr", 0, 129)])
         ts(T.ql[:], T.qx[:, 15:128:16], koc, A.subtract, [B("ql")], [B("qx"), B("kcol", 1, 2)])
         for b in range(4):
-            act(T.fqh[:, 128 * b:128 * b + 128], T.fs[:, 320 * b:320 * b + 320].indirect(T.ql[:, 0:8]), AF.Copy, [B("fqh", 128 * b, 128 * b + 128)], [B("fs", 320 * b, 320 * b + 320), B("ql")])
-        tt(T.e1[:], T.qr[:, 0:128], T.qr[:, 1:129], A.is_equal, [B("e1")], [B("qr", 0, 129)])
+            o, i = T.fqh[:, 128 * b:128 * b + 128], T.fs[:, 320 * b:320 * b + 320].indirect(T.ql[:, 0:8])
+            w, r = [B("fqh", 128 * b, 128 * b + 128)], [B("fs", 320 * b, 320 * b + 320), B("ql")]
+            if b < 2:
+                act(o, i, AF.Copy, w, r)
+            else:
+                cp(o, i, w, r)
         tt(T.e2[:], T.e1[:], k_("dk"), A.mult, [B("e2")], [B("e1"), B("dk")])
         for b in range(4):
             tt(T.vt[:, b:512:4], T["pb%d" % (2 + b)][:, 0:128], T.fqh[:, 128 * b:128 * b + 128], A.add, [B("vt", 0, 512, b)], [B("pb%d" % (2 + b)), B("fqh", 128 * b, 128 * b + 128)])
@@ -387,14 +432,12 @@ def rank_program(g, core, T, topo):
         tt(T.oq[:], T.orow[:, 0:320].indirect(T.ql[:, 0:8]), T.e2[:], A.max, [B("oq")], [B("orow"), B("ql"), B("e2")])
         diag(T.oqx[:], T.oq[:], 128, [B("oqx")], [B("oq")])
         for b in range(4):
-            ts(T.xl[:, 8 * b:8 * b + 8], T.oqx[:, 15:128:16], ko, A.subtract, [B("xl", 8 * b, 8 * b + 8)], [B("oqx"), B("kcol", 0, 1)], float(b), A.add)
-        for b in range(4):
             d = slice(128 * b, 128 * b + 128)
             tt(T.tb[:, d], T["pb%d" % (2 + b)][:, 0:128], T.fq32[:, d], A.add, [B("tb", d.start, d.stop)], [B("pb%d" % (2 + b)), B("fq32")])
             act(T.nb[:, d], T.tb[:, d], AF.Copy, [B("nb", d.start, d.stop)], [B("tb", d.start, d.stop)], scale=0.0625)
+        for b in range(4):
+            ts(T.xl[:, 8 * b:8 * b + 8], T.oqx[:, 15:128:16], ko, A.subtract, [B("xl", 8 * b, 8 * b + 8)], [B("oqx"), B("kcol", 0, 1)], float(b), A.add)
         cp(T.xw[:, 0:1792].indirect(T.xl[:, 0:32]), T.nb[:], [B("xw")], [B("nb"), B("xl")])
-        if t == 0:
-            quant("vv", "v0", 0, 128)
 
     quant("xx", "xw", 0, 320)
     mm(0, 320, "vv", 0, "xx")

from concourse.bass import DstId, RemoteDMATransfer, IndirectOffsetOnAxis
from concourse.mybir import dt, AluOpType, ActivationFunctionType as AF

C, K, R = 320, 128, 3
BIG = 1e25
M = 2048
UNITS = [[19, 18, 17, None], [16, 15, 14, 13], [12, 11, 10, 9], [8, 7, 6, 5], [4, 3, 2, 1]]
WIDTH = [320, 256, 192, 128, 128]

F8, U8, BF, F32, I32, U16 = "float8_e4m3fn_x4", "uint8", "bfloat16", "float32", "int32", "uint16"
SCRATCH = {}


def _b(name, cols, dtype):
    SCRATCH[name] = ("sbuf", [128, cols], dtype)


def _q(name, cols):
    _b("q" + name, cols, F8)
    _b("s" + name, cols, U8)


for _n, _c in (("xx", 320), ("uu", 128), ("ua", 128), ("ub", 128), ("vv", 128), ("ww", 512), ("vt", 128), ("bo", 128), ("bd", 128)):
    _q(_n, _c)
for _i in range(4):
    _q("ez%d" % _i, 128)
for _i in range(5):
    _q("ct%d" % _i, WIDTH[_i])
    _b("ct%d" % _i, 4 * WIDTH[_i], BF)
for _i in range(R):
    _q("eo%d" % _i, 128)
    _q("ei%d" % _i, 128)
    _b("pl%d" % _i, 8, U16)
    SCRATCH["lp%d" % _i] = ("dram", [256, 8], U16)
for _n, _c, _d in (
        ("x0", 1280, BF), ("xw", 1792, BF), ("u0", 512, BF), ("v0", 512, BF),
        ("half", 516, BF), ("zed", 516, BF), ("bot", 512, BF), ("bdt", 512, BF),
        ("rvi", 32, I32), ("rvf", 32, F32), ("rvt", 32, F32), ("rvr", 640, F32), ("rvc", 320, BF),
        ("mk0", 320, BF), ("mk1", 320, BF), ("scm", 320, F32), ("scf", 320, F32), ("dsum", 320, BF), ("junk", 3072, BF),
        ("fre", 20, F32), ("li", 192, F32), ("dg", 960, F32), ("rl", 64, U16),
        ("orow", 320, F32), ("ol", 80, U16), ("ar", 640, BF), ("bx", 336, BF), ("bs", 1280, BF),
        ("fs", 1280, BF), ("fa", 512, BF), ("zr", 640, BF), ("zx", 512, F32), ("zl", 32, U16), ("et", 512, BF),
        ("bxx", 960, F32), ("bl", 60, U16), ("tt", 960, BF), ("pls", 40, U16), ("qq", 512, BF), ("qr", 136, BF), ("qx", 128, F32), ("ql", 8, U16),
        ("fqh", 512, F32), ("vt", 512, BF), ("fq32", 512, F32), ("e1", 128, BF), ("e2", 128, F32), ("oq", 128, F32), ("oqx", 128, F32),
        ("xl", 32, U16), ("tb", 512, F32), ("nb", 512, BF), ("yo", 320, F32)):
    _b(_n, _c, _d)
ALIAS = {}
for _buf, _d, _l in (
        ("kf", F32, (("iprow", 320), ("eqm", 320), ("gtm", 320), ("mb", 320), ("cb", 320), ("rsm", 320), ("rst", 320), ("iota4", 320), ("grow", 512), ("dk", 128),
                     ("c20", 20), ("cl", 20), ("n20", 20), ("n8", 8), ("na", 8), ("nb8", 8), ("icol", 4), ("gcol", 4), ("gpc", 4), ("kcol", 4))),
        ("ki", I32, (("pidx", 4), ("pi15", 4), ("pi4", 4), ("pi5", 4), ("pi41", 4))),
        ("kb", BF, (("idc", 320), ("drm", 320), ("p0r", 128), ("neg", 320))),
        ("kl", U16, (("ula", 8), ("ulb", 8), ("rev8", 8), ("rev20", 20)))):
    _o = 0
    for _n, _c in _l:
        ALIAS[_n] = (_buf, _o, _c)
        _o += (_c + 15) // 16 * 16
    _b(_buf, _o, _d)
SCRATCH["rvd"] = ("dram", [4, 640], F32)
for _i in range(8):
    SCRATCH["pb%d" % _i] = ("psum", [128, 512], F32)

SEMAPHORES = ["kv", "ks", "kt", "kp", "ls", "dx", "du", "dv", "dr", "dw", "drd", "dri", "dp", "db1", "db2", "db3", "db4", "dq", "do", "dy"]
SEMAPHORES += ["ap%d" % i for i in range(R)] + ["ae%d" % i for i in range(R)]


def rank_program(g, core, T, topo):
    rank = T.rank_of(core)
    if rank is None:
        return
    A = AluOpType
    nxt = T.cores[(rank + 1) % len(T.cores)]
    rid, pid, _s = topo.addr(nxt)
    eng = topo.engines(core, nxt)[:8]
    ne, mask = len(eng), sum(1 << e for e in eng)

    queues = {"v": g.vector, "s": g.scalar, "t": g.tensor, "p": g, "y": g.sync}
    own = {"v": "kv", "s": "ks", "t": "kt", "p": "kp"}
    total, seen, hist = {}, {q: {} for q in queues}, {}

    def wait(q, sem, val):
        if seen[q].get(sem, 0) < val:
            queues[q].wait_ge(T.sem[sem], val)
            seen[q][sem] = val

    def k_(name, lo=0, hi=None):
        buf, o, n = ALIAS[name]
        return T[buf][:, o + lo:o + (n if hi is None else hi)]

    def B(name, lo=0, hi=None, ph=None):
        if name in ALIAS:
            buf, o, n = ALIAS[name]
            return (buf, o + lo, o + (n if hi is None else hi), ph)
        return (name, lo, SCRATCH[name][1][1] if hi is None else hi, ph)

    def clash(a, rec):
        return a[1] < rec[1] and rec[0] < a[2] and (a[3] is None or rec[2] is None or a[3] == rec[2])

    def deps(q, rd, wr):
        need = {}
        for accs, w in ((rd, False), (wr, True)):
            for a in accs:
                bank = a[0][:2] == "pb"
                for rec in hist.get(a[0], []):
                    if bank and q != rec[5] or clash(a, rec) and (w or rec[3]):
                        if q == "t" and rec[5] == "t":
                            continue
                        need[rec[4][0]] = max(need.get(rec[4][0], 0), rec[4][1])
        for s in sorted(need):
            wait(q, s, need[s])

    def note(q, rd, wr, tok):
        for a in rd:
            hist.setdefault(a[0], []).append((a[1], a[2], a[3], False, tok, q))
        for a in wr:
            h = hist.setdefault(a[0], [])
            h[:] = [x for x in h if not (a[1] <= x[0] and x[1] <= a[2] and (a[3] is None or a[3] == x[2]) and x[4] != tok)]
            h.append((a[1], a[2], a[3], True, tok, q))

    def op(q, fn, args, rd, wr, **kw):
        deps(q, rd, wr)
        sem = own[q]
        fn(*args, **kw).then_inc(T.sem[sem], 1)
        total[sem] = total.get(sem, 0) + 1
        note(q, rd, wr, (sem, total[sem]))

    def dmas(q, sem, items):
        for o, i, rd, wr in items:
            deps(q, rd, wr)
            queues[q].dma_start(o, i).then_inc(T.sem[sem], 16)
            total[sem] = total.get(sem, 0) + 16
        for o, i, rd, wr in items:
            note(sem, rd, wr, (sem, total[sem]))

    v, s = g.vector, g.scalar

    def ts(out, in0, s1, op0, wr, rd, s2=None, op1=None):
        if op1 is None:
            op("v", v.tensor_scalar, (out, in0, s1, None, op0), rd, wr)
        else:
            op("v", v.tensor_scalar, (out, in0, s1, s2, op0, op1), rd, wr)

    def tt(out, a, b, o, wr, rd):
        op("v", v.tensor_tensor, (out, a, b, o), rd, wr)

    def scan(out, d0, d1, init, o0, o1, wr, rd):
        op("v", v.tensor_tensor_scan, (out, d0, d1, init, o0, o1), rd, wr)

    def cp(out, i, wr, rd):
        op("v", v.tensor_copy, (out, i), rd, wr)

    def act(out, i, func, wr, rd, **kw):
        op("s", s.activation, (out, i, func), rd, wr, **kw)

    def ms(name, lo, hi, val):
        op("v", v.memset, (T[name][:, lo:hi], val), [], [B(name, lo, hi)])

    def quant(name, tname, lo, n):
        op("v", v.quantize_mx, (T["q" + name][:, 0:n], T["s" + name][:, 0:n], T[tname][:, lo:lo + 4 * n]),
           [B(tname, lo, lo + 4 * n)], [B("q" + name, 0, n), B("s" + name, 0, n)])

    def mm(bank, n, st, sa, mv, start=True, stop=True):
        op("t", g.tensor.matmul_mx, (T["pb%d" % bank][:, 0:n], T["q" + st][:, sa:sa + 128], T["s" + st][:, sa:sa + 128],
                                     T["q" + mv][:, 0:n], T["s" + mv][:, 0:n], start, stop),
           [B("q" + st), B("s" + st), B("q" + mv), B("s" + mv)], [B("pb%d" % bank)])

    def iota(name, pat, base, cm, n):
        op("p", g.iota, (k_(name, 0, n), pat, base, cm), [], [B(name, 0, n)], allow_small_or_imprecise_dtypes=True)

    def diag(out, row, n, wr, rd):
        scan(out, k_("cb", 0, n), row, 0.0, A.add, A.max, wr, rd + [B("cb", 0, n)])

    dmas("y", "dx", [(T.x0[:], T.x[:], [], [B("x0")])])
    dmas("s", "du", [(T.u0[:], T.u[:], [], [B("u0")])])
    dmas("y", "dr", [(T.rvi[:, 0:20], T.rv[:], [], [B("rvi", 0, 20)])])
    dmas("y", "dw", [(T.qww[:, 0:512].bitcast(dt.uint8), T.wc[:], [], [B("qww")]), (T.sww[:, 0:512], T.ws[:], [], [B("sww")])])
    dmas("y", "dv", [(T.v0[:], T.v[:], [], [B("v0")])])

    op("p", g.iota, (k_("pidx", 0, 1), [[0, 1]], 0, 1), [], [B("pidx")])
    iota("na", [[16, 8]], 0, 0, 8)
    iota("nb8", [[16, 8]], 8, 0, 8)
    iota("iprow", [[0, 20], [1, 16]], 0, 0, 320)
    ms("half", 0, 516, 0.5)
    iota("grow", [[1, 8], [0, 64]], 0, 0, 512)
    op("p", g.affine_select, (T.zed[:], T.half[:], [[1, 516]], A.is_equal, 0.0, -3, -4), [B("half")], [B("zed")])
    iota("c20", [[16, 20]], 0, 0, 20)
    iota("n20", [[-32, 20]], 623, 0, 20)
    iota("n8", [[-16, 8]], 127, 0, 8)
    iota("iota4", [[4, 320]], 0, 0, 320)
    iota("p0r", [[2, 128]], -159, 0, 128)
    iota("idc", [[1, 320]], -160, 0, 320)
    iota("dk", [[4, 128]], 1280, 0, 128)

    def c1(name, j=0):
        return k_(name, j, j + 1), [B(name, j, j + 1)]

    def kts(o, i, s1, op0, s2=None, op1=None, extra=()):
        ts(o[0], i[0], s1, op0, o[1], i[1] + list(extra), s2, op1)

    def kw(name):
        return k_(name), [B(name)]
    kts(c1("pi15"), c1("pidx"), 15, A.bitwise_and)
    kts(c1("pi5"), c1("pidx"), 5, A.arith_shift_right)
    kts(c1("pi4"), c1("pidx"), 4, A.arith_shift_right)
    cp(k_("ula"), k_("na"), [B("ula")], [B("na")])
    cp(k_("ulb"), k_("nb8"), [B("ulb")], [B("nb8")])
    cp(c1("icol")[0], c1("pi15")[0], c1("icol")[1], c1("pi15")[1])
    cp(c1("gcol")[0], c1("pi4")[0], c1("gcol")[1], c1("pi4")[1])
    kts(c1("pi41"), c1("pi4"), 1, A.bitwise_and)
    cp(c1("gpc")[0], c1("pi41")[0], c1("gpc")[1], c1("pi41")[1])
    ic, icr = c1("icol")
    kts(c1("kcol"), c1("icol"), -float(M), A.mult, 15.0 * M, A.add)
    kts(c1("kcol", 1), c1("icol"), -float(M), A.mult, 15.0 * M - 160.0, A.add)
    kts(c1("kcol", 2), c1("icol"), M + 1.0, A.mult, -15.0 * M, A.add)
    kts(c1("gpc", 1), c1("gpc"), 16.0, A.mult, ic, A.subtract, icr)
    ko, koc = k_("kcol", 0, 1), k_("kcol", 1, 2)
    kts(kw("eqm"), kw("iprow"), ic, A.is_equal, extra=icr)
    kts(kw("drm"), kw("iprow"), 0.0, A.is_gt)
    kts(kw("gtm"), kw("iprow"), ic, A.is_gt, float(M), A.mult, icr)
    act(k_("rst"), k_("eqm"), AF.Copy, [B("rst")], [B("eqm")], scale=-1e6)
    act(k_("mb"), k_("eqm"), AF.Copy, [B("mb")], [B("eqm")], scale=2 * BIG, bias=-BIG)
    act(k_("rsm"), k_("drm"), AF.Copy, [B("rsm")], [B("drm")], scale=2 * BIG, bias=-BIG)
    for i in range(5):
        ms("ct%d" % i, 64 * min(a for a in UNITS[i] if a), 4 * WIDTH[i], 0.0)
    ts(T.bot[:], k_("grow"), k_("gcol", 0, 1), A.is_equal, [B("bot")], [B("grow"), B("gcol", 0, 1)])
    act(T.bdt[:], T.bot[:], AF.Copy, [B("bdt")], [B("bot")])
    act(T.bdt[:, 3:512:4], T.bot[:, 3:512:4], AF.Copy, [B("bdt")], [B("bot")], scale=-1.0)
    quant("uu", "u0", 0, 128)
    for d, l in (("ua", "ula"), ("ub", "ulb")):
        cp(T["q" + d][:, 0:128].bitcast(dt.uint32), T.quu[:, 0:128].bitcast(dt.uint32).indirect(k_(l)), [B("q" + d)], [B("quu"), B(l)])
        act(T["s" + d][:, 0:128], T.suu[:, 0:128].indirect(k_(l)), AF.Copy, [B("s" + d)], [B("suu"), B(l)])

    def late_constants():
        tt(k_("cb"), k_("rst"), k_("gtm"), A.add, [B("cb")], [B("rst"), B("gtm")])
        quant("bo", "bot", 0, 128)
        quant("bd", "bdt", 0, 128)
        kts(kw("cl"), kw("c20"), k_("kcol", 2, 3), A.add, extra=[B("kcol", 2, 3)])
        kts(kw("rev8"), kw("n8"), ic, A.subtract, extra=icr)
        kts(kw("rev20"), kw("n20"), k_("gpc", 1, 2), A.add, extra=[B("gpc", 1, 2)])
        ms("fre", 0, 1, 0.0)
        ms("bx", 0, 1, -160.0)
        ms("qr", 128, 136, 512.0)
        op("v", v.memset, (k_("neg"), -512.0), [], [B("neg")])

    ms("rvi", 20, 32, 0)
    ts(T.rvf[:], T.rvi[:], 1.0, A.max, [B("rvf")], [B("rvi")], -1.0, A.mult)
    op("v", v.transpose, (T.rvt[:], T.rvf[:]), [B("rvf")], [B("rvt")])
    dmas("y", "drd", [(T.rvd[b:b + 1, :], T.rvt[32 * b:32 * b + 20, 0:32], [B("rvt")], [("rvd", b, b + 1, None)]) for b in range(4)])
    deps("p", [("rvd", 0, 4, None), B("pi5")], [B("rvr")])
    g.indirect_dma_start(T.rvr[:, 0:640], None, T.rvd[:], IndirectOffsetOnAxis(ap=k_("pi5", 0, 1), axis=0), bounds_check=3, oob_is_err=True).then_inc(T.sem["dri"], 16)
    total["dri"] = 16
    note("dri", [("rvd", 0, 4, None), B("pi5")], [B("rvr")], ("dri", 16))

    def scores():
        mm(0, 320, "ua", 0, "xx")
        mm(1, 320, "ub", 0, "xx")

    for t in range(R):
        quant("xx", "x0" if t == 0 else "xw", 0, 320)
        scores()
        if t == 0:
            late_constants()
        tt(T.scm[:], T.pb0[:, 0:320], k_("mb"), A.min, [B("scm")], [B("pb0"), B("mb")])
        if t == 0:
            for b in range(2):
                quant("ez%d" % b, "zed", 3 - b, 128)
        scan(T.scf[:], k_("rsm"), T.scm[:], -BIG, A.min, A.max, [B("scf")], [B("rsm"), B("scm")])
        if t == 0:
            for b in range(2, 4):
                quant("ez%d" % b, "zed", 3 - b, 128)
        for b in range(4):
            mm(2 + b, 320, "ez%d" % b, 0, "xx")
        act(T.mk0[:], T.pb1[:, 0:320], AF.Sign, [B("mk0")], [B("pb1")])
        act(T.mk1[:], T.mk0[:], AF.Relu, [B("mk1")], [B("mk0")])

        def whole(b):
            act(T.xw[:, b:1280:4], T["pb%d" % (2 + b)][:, 0:320], AF.Copy, [B("xw", 0, 1280, b)], [B("pb%d" % (2 + b))], scale=2.0)
        whole(0)
        off = 0

        def li(j):
            return T.li[:, 32 * j:32 * j + 20], B("li", 32 * j, 32 * j + 20)

        def count(i):
            quant("ct%d" % i, "ct%d" % i, 0, WIDTH[i])
            mm(6, WIDTH[i], "bd" if i == 0 else "bo", 0, "ct%d" % i, i == 0, i == 4)
        for i in range(5):
            ct = "ct%d" % i
            for k, a in enumerate(UNITS[i]):
                if i and k == 1:
                    count(i - 1)
                if a is None:
                    tt(T[ct][:, k:1280:4], T.scf[:], T.pb0[:, 0:320], A.is_ge, [B(ct, 0, 1280, k)], [B("scf"), B("pb0")])
                    continue
                n = 16 * a
                ts(T[ct][:, k:4 * n:4], T.pb0[:, 0:n], T.scf[:, n + 15:n + 16], A.is_ge, [B(ct, 0, 4 * n, k)], [B("pb0"), B("scf")])
                act(T.junk[:, off:off + n], T[ct][:, k:4 * n:4], AF.Copy, [B("junk", off, off + n), B("fre", a, a + 1)], [B(ct, 0, 4 * n, k)],
                    accum_out=T.fre[:, a:a + 1])
                off += n
            if i == 1:
                scan(T.dsum[:], k_("drm"), T.ct0[:, 3:1280:4], 0.0, A.mult, A.add, [B("dsum")], [B("drm"), B("ct0", 0, 1280, 3)])
            if i == 2:
                tt(li(0)[0], T.dsum[:, 15:320:16], k_("cl"), A.add, [li(0)[1]], [B("dsum"), B("cl")])
        diag(T.dg[:, 320:640], T.mk1[:], 320, [B("dg", 320, 640)], [B("mk1")])
        count(4)
        if t == 0:
            ts(T.rvc[:], T.rvr[:, 0:640].indirect(k_("rev20")), 160.0, A.add, [B("rvc")], [B("rvr"), B("rev20")])
        act(T.ar[:, 0:320], T.rvc[:], AF.Copy, [B("ar", 0, 320)], [B("rvc")])
        for b in range(1, 4):
            whole(b)
        ts(li(3)[0], T.dg[:, 335:640:16], ko, A.subtract, [li(3)[1]], [B("dg", 320, 640), B("kcol", 0, 1)], 320.0, A.mult)
        tt(li(1)[0], li(0)[0], T.fre[:], A.subtract, [li(1)[1]], [li(0)[1], B("fre")])
        tt(li(2)[0], li(1)[0], li(3)[0], A.add, [li(2)[1]], [li(1)[1], li(3)[1]])
        diag(T.dg[:, 0:320], T.pb6[:, 0:320], 320, [B("dg", 0, 320)], [B("pb6")])
        tt(li(4)[0], T.dg[:, 15:320:16], li(2)[0], A.add, [li(4)[1]], [B("dg", 0, 320), li(2)[1]])
        tt(li(5)[0], T.dg[:, 15:320:16], li(1)[0], A.add, [li(5)[1]], [B("dg", 0, 320), li(1)[1]])
        cp(T.rl[:, 32:52], li(4)[0], [B("rl", 32, 52)], [li(4)[1]])
        cp(T.rl[:, 0:20], li(5)[0], [B("rl", 0, 20)], [li(5)[1]])
        cp(T.ar[:, 0:640].indirect(T.rl[:, 32:52]), k_("neg"), [B("ar")], [B("neg"), B("rl", 32, 52)])
        scan(T.bx[:, 1:320], T.ar[:, 0:319], T.ar[:, 0:319], -160.0, A.max, A.max, [B("bx", 1, 320)], [B("ar", 0, 320)])
        for j in (4, 3, 2, 1):
            c = 320 * (j - 1)
            h = 16 * j
            dmas("y", "db%d" % j, [
                (T.bs[h:128, c:c + 320], T.bx[0:128 - h, 0:320], [B("bx", 0, 320)], [B("bs", c, c + 320, 0)]),
                (T.bs[0:h, c:c + 320], T.bx[128 - h:128, 0:320], [B("bx", 0, 320)], [B("bs", c, c + 320, 1)])])
        cp(T.orow[:, 0:320].indirect(T.rl[:, 0:20]), k_("iota4"), [B("orow")], [B("iota4"), B("rl", 0, 20)])
        diag(T.dg[:, 640:960], T.orow[:], 320, [B("dg", 640, 960)], [B("orow")])
        for b in range(4):
            ts(T.ol[:, 20 * b:20 * b + 20], T.dg[:, 655:960:16], ko, A.subtract, [B("ol", 20 * b, 20 * b + 20)], [B("dg", 640, 960), B("kcol", 0, 1)], float(b), A.add)

        def ordered(b):
            f = 320 * b
            act(T.fs[:, f:f + 320], T.xw[:, 0:1280].indirect(T.ol[:, 20 * b:20 * b + 20]), AF.Copy, [B("fs", f, f + 320)], [B("xw", 0, 1280), B("ol", 20 * b, 20 * b + 20)], scale=0.5)
            act(T.fa[:, 128 * b:128 * b + 128], T.fs[:, f + 1:f + 257:2], AF.Copy, [B("fa", 128 * b, 128 * b + 128)], [B("fs", f, f + 320)])

        def bs(j):
            return T.bs[:, 320 * (j - 1):320 * j], B("bs", 320 * (j - 1), 320 * j)
        def table_row(n, j):
            diag(T.bxx[:, 320 * n:320 * n + 320], bs(j)[0], 320, [B("bxx", 320 * n, 320 * n + 320)], [bs(j)[1]])

        def table_list(n):
            ts(T.bl[:, 20 * n:20 * n + 20], T.bxx[:, 320 * n + 15:320 * n + 320:16], koc, A.subtract, [B("bl", 20 * n, 20 * n + 20)], [B("bxx", 320 * n, 320 * n + 320), B("kcol", 1, 2)])

        def compose(n):
            src, sr = bs(1) if n == 0 else (T.tt[:, 320 * n - 320:320 * n], B("tt", 320 * n - 320, 320 * n))
            act(T.tt[:, 320 * n:320 * n + 320], src.indirect(T.bl[:, 20 * n:20 * n + 20]), AF.Copy, [B("tt", 320 * n, 320 * n + 320)], [sr, B("bl", 20 * n, 20 * n + 20)])

        def zrow(n):
            return T.zr[:, 128 * n:128 * n + 128], B("zr", 128 * n, 128 * n + 128)

        def zdiag(n):
            diag(T.zx[:, 128 * n:128 * n + 128], zrow(n)[0], 128, [B("zx", 128 * n, 128 * n + 128)], [zrow(n)[1]])

        def zlist(n):
            o, w = (T.zl[:, 8 * n:8 * n + 8], [B("zl", 8 * n, 8 * n + 8)]) if n < 2 else (T["pl%d" % t][:], [B("pl%d" % t)])
            ts(o, T.zx[:, 128 * n + 15:128 * n + 128:16], koc, A.subtract, w, [B("zx", 128 * n, 128 * n + 128), B("kcol", 1, 2)])
        p0 = (k_("p0r"), B("p0r"))
        ordered(0)
        ordered(1)
        tt(zrow(0)[0], T.bs[:, 961:1217:2], p0[0], A.max, [zrow(0)[1]], [bs(4)[1], p0[1]])
        table_row(0, 2)
        zdiag(0)
        table_list(0)
        compose(0)
        ordered(2)
        ordered(3)
        zlist(0)
        tt(zrow(3)[0], T.bs[:, 1:257:2], p0[0], A.max, [zrow(3)[1]], [bs(1)[1], p0[1]])
        tt(zrow(1)[0], bs(3)[0].indirect(T.zl[:, 0:8]), p0[0], A.max, [zrow(1)[1]], [bs(3)[1], B("zl", 0, 8), p0[1]])
        zdiag(1)
        zlist(1)
        tt(zrow(2)[0], T.tt[:, 0:320].indirect(T.zl[:, 8:16]), zrow(3)[0], A.max, [zrow(2)[1]], [B("tt", 0, 320), B("zl", 8, 16), zrow(3)[1]])
        zdiag(2)
        zlist(2)
        pl = T["pl%d" % t]
        lp = T["lp%d" % t]
        dst = DstId(rid=rid, pnc=pid)
        deps("p", [B("pl%d" % t)], [])
        g.remote_dma_fused([RemoteDMATransfer(dst_ids=[dst, dst], dma_engine_mask=mask, remote_sem=T.sem["ap%d" % t], srcs=[pl[:]], dsts=[lp[0:128, :], lp[128:256, :]])],
                           local_sem=T.sem.ls)
        note("ap%d" % t, [], [B("lp%d" % t, 0, 8)], ("ap%d" % t, 2 * ne))
        total["ap%d" % t] = 2 * ne
        for b in range(4):
            f = 320 * b
            tt(T.et[:, b:512:4], T.fs[:, f:f + 320].indirect(pl[:, 0:8]), T.fa[:, 128 * b:128 * b + 128], A.add, [B("et", 0, 512, b)], [B("fs", f, f + 320), B("fa", 128 * b, 128 * b + 128), B("pl%d" % t)])
        quant("eo%d" % t, "et", 0, 128)
        qo, so = "qeo%d" % t, "seo%d" % t
        deps("p", [B(qo), B(so)], [])
        g.remote_dma(T["qei%d" % t][:, 0:128].bitcast(dt.uint8), T[qo][:, 0:128].bitcast(dt.uint8), T.sem["ae%d" % t], T.sem.ls, pid, rid, mask)
        g.remote_dma(T["sei%d" % t][:, 0:128], T[so][:, 0:128], T.sem["ae%d" % t], T.sem.ls, pid, rid, mask)
        note("ae%d" % t, [], [B("qei%d" % t), B("sei%d" % t)], ("ae%d" % t, 2 * ne))
        total["ae%d" % t] = 2 * ne
        total["ls"] = total.get("ls", 0) + 3 * ne
        table_row(1, 3)
        table_row(2, 4)
        for n in (1, 2):
            table_list(n)
            compose(n)
        if t == 0:
            quant("vv", "v0", 0, 128)
        dmas("y", "dp", [(T.pls[:, 8 * j:8 * j + 8], lp[128 - 16 * j:256 - 16 * j, :], [B("lp%d" % t)], [B("pls", 8 * j, 8 * j + 8)]) for j in range(5)])
        for b in range(4):
            mm(2 + b, 128, "ez%d" % b, 0, "ei%d" % t)
        prev = None
        for n, (src, sr) in enumerate(((T.tt[:, 640:960], B("tt", 640, 960)), (T.tt[:, 320:640], B("tt", 320, 640)), (T.tt[:, 0:320], B("tt", 0, 320)), bs(1), (k_("idc"), B("idc")))):
            l = 8 * (4 - n)
            o, w = (T.qq[:, 128 * n:128 * n + 128], B("qq", 128 * n, 128 * n + 128)) if n < 4 else (T.qr[:, 0:128], B("qr", 0, 128))
            i = src.indirect(T.pls[:, l:l + 8])
            if prev is None:
                cp(o, i, [w], [sr, B("pls", l, l + 8)])
            else:
                tt(o, i, prev[0], A.max, [w], [sr, B("pls", l, l + 8), prev[1]])
            prev = (o, w)
        diag(T.qx[:], T.qr[:, 0:128], 128, [B("qx")], [B("qr", 0, 128)])
        tt(T.e1[:], T.qr[:, 0:128], T.qr[:, 1:129], A.is_equal, [B("e1")], [B("qr", 0, 129)])
        ts(T.ql[:], T.qx[:, 15:128:16], koc, A.subtract, [B("ql")], [B("qx"), B("kcol", 1, 2)])
        for b in range(4):
            o, i = T.fqh[:, 128 * b:128 * b + 128], T.fs[:, 320 * b:320 * b + 320].indirect(T.ql[:, 0:8])
            w, r = [B("fqh", 128 * b, 128 * b + 128)], [B("fs", 320 * b, 320 * b + 320), B("ql")]
            if b < 2:
                act(o, i, AF.Copy, w, r)
            else:
                cp(o, i, w, r)
        tt(T.e2[:], T.e1[:], k_("dk"), A.mult, [B("e2")], [B("e1"), B("dk")])
        for b in range(4):
            tt(T.vt[:, b:512:4], T["pb%d" % (2 + b)][:, 0:128], T.fqh[:, 128 * b:128 * b + 128], A.add, [B("vt", 0, 512, b)], [B("pb%d" % (2 + b)), B("fqh", 128 * b, 128 * b + 128)])
        quant("vt", "vt", 0, 128)
        for b in range(4):
            mm(2 + b, 128, "ww", 128 * b, "vt")
        act(T.fq32[:], T.fqh[:], AF.Copy, [B("fq32")], [B("fqh")], scale=32.0)
        tt(T.oq[:], T.orow[:, 0:320].indirect(T.ql[:, 0:8]), T.e2[:], A.max, [B("oq")], [B("orow"), B("ql"), B("e2")])
        diag(T.oqx[:], T.oq[:], 128, [B("oqx")], [B("oq")])
        for b in range(4):
            d = slice(128 * b, 128 * b + 128)
            tt(T.tb[:, d], T["pb%d" % (2 + b)][:, 0:128], T.fq32[:, d], A.add, [B("tb", d.start, d.stop)], [B("pb%d" % (2 + b)), B("fq32")])
            act(T.nb[:, d], T.tb[:, d], AF.Copy, [B("nb", d.start, d.stop)], [B("tb", d.start, d.stop)], scale=0.0625)
        for b in range(4):
            ts(T.xl[:, 8 * b:8 * b + 8], T.oqx[:, 15:128:16], ko, A.subtract, [B("xl", 8 * b, 8 * b + 8)], [B("oqx"), B("kcol", 0, 1)], float(b), A.add)
        cp(T.xw[:, 0:1792].indirect(T.xl[:, 0:32]), T.nb[:], [B("xw")], [B("nb"), B("xl")])

    quant("xx", "xw", 0, 320)
    mm(0, 320, "vv", 0, "xx")
    ts(T.tb[:, 0:128], T.qr[:, 0:128].indirect(k_("rev8")), -1.0, A.mult, [B("tb", 0, 128)], [B("qr", 0, 128), B("rev8")], 159.0, A.add)
    dmas("y", "do", [(T.oc[:], T.qxx[:, 0:320].bitcast(dt.uint8), [B("qxx")], [])]
         + [(T.osc[4 * k:4 * k + 4, :], T.sxx[32 * k:32 * k + 4, 0:320], [B("sxx")], []) for k in range(4)]
         + [(T.lq[:], T.tb[0:128:16, 0:128], [B("tb", 0, 128)], [])])
    act(T.yo[:], T.pb0[:, 0:320], AF.Copy, [B("yo")], [B("pb0")])
    dmas("s", "dy", [(T.y[:], T.yo[:], [B("yo")], [])])
    for sem in sorted(total):
        wait("p", sem, total[sem])
